import numpy as np
import ml_dtypes


def mxq(x, axis, fmt="e4m3"):
    dtype, down = {"e4m3": (ml_dtypes.float8_e4m3fn, 7), "e5m2": (ml_dtypes.float8_e5m2, 14)}[fmt]
    v = np.moveaxis(np.asarray(x, np.float32).astype(ml_dtypes.bfloat16).astype(np.float64), axis, -1)
    blocks = v.reshape(v.shape[:-1] + (-1, 32))
    amax = np.abs(blocks).max(-1, keepdims=True)
    byte = np.maximum(np.where(amax > 0, np.frexp(amax)[1] - 1 + 127, 0) - down, 1)
    scale = np.exp2(byte - 127.0)
    codes = (blocks / scale).astype(np.float32).astype(dtype).astype(np.float64)
    return np.moveaxis((codes * scale).reshape(v.shape), -1, axis)


WIDE = False


def mx_kscale(k):
    if not WIDE:
        return np.ones(k)
    levels = np.array([10, -10, 5, -5, 0])
    if k % 512:
        return np.exp2(np.random.permutation(np.resize(levels, k // 32))).repeat(32)
    a = np.empty((k // 512, 16))
    for p in range(k // 512):
        a[p, :8] = np.random.permutation(np.resize(levels, 8))
        for g in range(8):
            far = levels[np.abs(levels - a[p, g]) >= 10]
            a[p, g + 8] = far[np.random.randint(len(far))]
    return np.exp2(a.ravel()).repeat(32)


BF16 = ml_dtypes.bfloat16


def bf(x):
    return np.asarray(x, np.float32).astype(BF16)


def f64(x):
    return np.asarray(x).astype(np.float64)


E2M1 = np.array([0.0, 0.5, 1.0, 1.5, 2.0, 3.0, 4.0, 6.0, -0.0, -0.5, -1.0, -1.5, -2.0, -3.0, -4.0, -6.0])


def pack_weight(w, fmt):
    k, n = w.shape
    w = f64(bf(w)).reshape(k // 32, 32, n)
    amax = np.abs(w).max(1)
    if fmt == "e4m3":
        byte = np.frexp(amax)[1] - 1 + 127 - 7
    else:
        mant, ex = np.frexp(amax / 6.0)
        byte = np.where(mant > 0.5, ex, ex - 1) + 127
    byte = np.clip(np.where(amax > 0, byte, 1), 1, 254)
    scaled = (w * np.exp2(127.0 - byte)[:, None, :]).reshape(k, n).astype(np.float32)
    by_word = np.ascontiguousarray(scaled.reshape(k // 512, 128, 4, n).transpose(0, 1, 3, 2))
    if fmt == "e4m3":
        words = by_word.astype(ml_dtypes.float8_e4m3fn).view(np.uint8)
    else:
        c = by_word.astype(ml_dtypes.float4_e2m1fn).view(np.uint8) & 0xF
        words = c[..., 0::2] | (c[..., 1::2] << 4)
    return np.ascontiguousarray(words), np.ascontiguousarray(byte.astype(np.uint8).reshape(k // 512, 16, n))


def unpack_weight(words, scales, fmt):
    g, p, n, _ = words.shape
    if fmt == "e4m3":
        vals = np.ascontiguousarray(words).view(ml_dtypes.float8_e4m3fn).astype(np.float64)
    else:
        nib = np.empty((g, p, n, 4), np.uint8)
        nib[..., 0::2] = words & 0xF
        nib[..., 1::2] = words >> 4
        vals = E2M1[nib]
    vals = vals * np.repeat(np.exp2(scales.astype(np.float64) - 127.0), 8, axis=1)[..., None]
    return vals.transpose(0, 1, 3, 2).reshape(g * 512, n)
def pack4(w):
    words, scales = pack_weight(w, "e2m1")
    return words.reshape(words.shape[0], 128, -1), scales


def unpack4(words, scales):
    return unpack_weight(words.reshape(words.shape[0], 128, -1, 2), scales, "e2m1")


def planes(Y):
    n, m = Y.shape
    b = f64(bf(Y)).reshape(n // 32, 32, m)
    amax = np.abs(b).max(1)
    byte = np.clip(np.where(amax > 0, np.frexp(amax)[1] - 1 + 127 - 7, 1), 1, 254)
    codes = (b * np.exp2(127.0 - byte)[:, None, :]).reshape(n, m).astype(np.float32).astype(ml_dtypes.float8_e4m3fn).view(np.uint8)
    words = codes.reshape(n // 512, 128, 4, m).transpose(0, 1, 3, 2)
    return np.ascontiguousarray(words), np.ascontiguousarray(byte.astype(np.uint8).reshape(n // 512, 16, m))


N_OBS, N_CTL, N_TRT = 2048, 512, 1536

COMMON, COL_SPREAD, ROW_SPREAD = 0.5, 0.5, 0.8


def setup_inputs():
    randn = np.random.randn
    s, t = mx_kscale(N_OBS), mx_kscale(N_CTL)
    shared = randn(N_OBS, 1)
    c = randn(N_OBS, N_CTL) + COMMON * shared * randn(1, N_CTL)
    c = f64(bf(c * np.exp(COL_SPREAD * randn(1, N_CTL)) / np.sqrt(N_CTL)))
    x = f64(bf(randn(N_OBS, N_TRT) + COMMON * shared * randn(1, N_TRT)))
    pinv = np.linalg.pinv(c)
    norms = np.sqrt((pinv ** 2).sum(axis=1))
    u = (pinv / norms[:, None]).T
    u_words, u_scales = pack4(u * s[:, None])
    z_words, z_scales = pack4(x / s[:, None])
    return {
        "u_words": u_words, "u_scales": u_scales,
        "z_words": z_words, "z_scales": z_scales,
        "norms": bf(norms * t),
        "controls": bf(c / t[None, :]),
        "treatments": bf(x),
        "row_weight": bf(np.exp(ROW_SPREAD * randn(N_OBS))),
    }


def reference(u_words, u_scales, z_words, z_scales, norms, controls, treatments, row_weight):
    u = unpack4(u_words, u_scales)
    z = unpack4(z_words, z_scales)
    coef = (u.T @ z) * f64(norms)[:, None]
    fitted = mxq(f64(controls), 1, "e4m3") @ mxq(coef, 0, "e4m3")
    y = (f64(treatments) - fitted) * f64(row_weight)[:, None]
    Y = y
    words, scales = planes(Y)
    return y, words, scales

@@ -1,0 +1,326 @@
+from contextlib import ExitStack
+
+import concourse.mybir as mybir
+from concourse.masks import make_identity
+
+N_OBS, N_CTL, N_TRT = 2048, 512, 1536
+FLOPS = 2 * N_OBS * N_CTL * N_TRT * 2
+
+F32 = mybir.dt.float32
+BF16 = mybir.dt.bfloat16
+I32 = mybir.dt.int32
+U32 = mybir.dt.uint32
+U8 = mybir.dt.uint8
+FP8X4 = mybir.dt.float8_e4m3fn_x4
+FP4X4 = mybir.dt.float4_e2m1fn_x4
+ALU = mybir.AluOpType
+COPY = mybir.ActivationFunctionType.Copy
+
+P = 128
+PACK = 4
+GROUP = P * PACK
+GROUPS = N_OBS // GROUP
+CHUNK = 512
+CHUNKS = N_TRT // CHUNK
+UNITS = [(0, 0), (1, 0), (0, 1), (1, 1), (0, 2), (1, 2), (2, 0), (2, 1), (2, 2), (3, 0), (3, 1), (3, 2)]
+
+
+def tile_frisch_waugh_partialling_k5_kernel(
+    tc, u_words, u_scales, z_words, z_scales, norms, controls, treatments, row_weight, out_0, out_1, out_2
+):
+    nc = tc.nc
+    with ExitStack() as ctx:
+        keep = ctx.enter_context(tc.tile_pool(name="keep", bufs=1))
+        turn = ctx.enter_context(tc.tile_pool(name="turn", bufs=2))
+        psum = ctx.enter_context(tc.psum_pool(name="psum", bufs=8))
+        ctx.enter_context(tc.manual_schedule())
+
+        def kept(name, shape, dtype):
+            return keep.tile(shape, dtype, name=name, align_bytes=64)
+
+        def bank(shape):
+            return psum.tile(shape, F32, name="bank")
+
+        def grouped_tile():
+            return turn.tile([P, CHUNK * PACK], BF16, name="grouped", bufs=4, align_bytes=64)
+
+        def cols(c):
+            return slice(c * CHUNK, (c + 1) * CHUNK)
+
+        def rows(g):
+            return slice(g * GROUP, (g + 1) * GROUP)
+
+        u_raw = kept("u_raw", [P, GROUPS, 2 * N_CTL], U8)
+        us_raw = kept("us_raw", [P, GROUPS, N_CTL], U8)
+        u_st = kept("u_st", [P, PACK, GROUPS, 2 * P], U8)
+        us_st = kept("us_st", [P, PACK, GROUPS, P], U8)
+        z_first = kept("z_first", [P, GROUPS, 2 * CHUNK], U8)
+        zs_first = kept("zs_first", [P, GROUPS, CHUNK], U8)
+        z_rest = kept("z_rest", [P, GROUPS, 2 * (N_TRT - CHUNK)], U8)
+        zs_rest = kept("zs_rest", [P, GROUPS, N_TRT - CHUNK], U8)
+        norms16 = kept("norms16", [P, PACK], BF16)
+        norms32 = kept("norms32", [P, PACK], F32)
+        w16 = kept("w16", [P, GROUPS, PACK], BF16)
+        w32 = kept("w32", [P, GROUPS, PACK], F32)
+        negw32 = kept("negw32", [P, GROUPS, PACK], F32)
+        ident = kept("ident", [P, P], F32)
+        coef16 = kept("coef16", [P, PACK, CHUNK], BF16)
+        coef_codes = [kept("coef_codes%d" % c, [P, CHUNK], U32) for c in range(CHUNKS)]
+        coef_scales = [kept("coef_scales%d" % c, [P, CHUNK], U8) for c in range(CHUNKS)]
+        ctl_codes = [kept("ctl_codes%d" % g, [P, GROUP], U32) for g in range(GROUPS)]
+        ctl_scales = [kept("ctl_scales%d" % g, [P, GROUP], U8) for g in range(GROUPS)]
+        y32 = [kept("y32_%d" % i, [P, PACK, CHUNK], F32) for i in range(len(UNITS))]
+        y_scales = kept("y_scales", [P, N_TRT], U8)
+        trt = {}
+        ctl_raw = {}
+        coef_bank = {}
+        ctl_bank = {}
+        fit_bank = {}
+        ctl_grouped = {}
+        coef_grouped = {}
+        y_grouped = {}
+        y_codes = {}
+
+        def load_scale_rows(plane, src, c0, c1, rs):
+            view = src.rearrange("g (q r) n -> r q g n", r=4)
+            for r in rs:
+                nc.sync.dma_start(out=plane[r:P:32].bitcast(I32), in_=view[r][:, :, c0:c1].bitcast(I32))
+
+        def load_words(dst, src, b0, b1):
+            nc.sync.dma_start(out=dst[:].bitcast(I32), in_=src.rearrange("g p b -> p g b")[:, :, b0:b1].bitcast(I32))
+
+        def load_controls(g):
+            ctl_raw[g] = turn.tile([P, PACK, N_CTL], BF16, name="ctl_raw", align_bytes=64)
+            nc.sync.dma_start(out=ctl_raw[g][:], in_=controls[rows(g), :].rearrange("(m t) k -> m t k", t=PACK))
+
+        def load_treatments(g, c0, c1):
+            tile = kept("trt_%d_%d" % (g, c0), [P, PACK, (c1 - c0) * CHUNK], BF16)
+            for c in range(c0, c1):
+                trt[g, c] = tile[:, :, (c - c0) * CHUNK : (c - c0 + 1) * CHUNK]
+            src = treatments[rows(g), c0 * CHUNK : c1 * CHUNK]
+            nc.sync.dma_start(out=tile[:], in_=src.rearrange("(p t) m -> p t m", t=PACK))
+
+        def order_u(t):
+            nc.vector.tensor_copy(
+                out=u_st[:, t].rearrange("p g (m b) -> p g m b", b=2),
+                in_=u_raw[:].rearrange("p g (m t b) -> p t g m b", t=PACK, b=2)[:, t],
+            )
+            nc.vector.tensor_copy(out=us_st[:, t], in_=us_raw[:].rearrange("p g (m t) -> p t g m", t=PACK)[:, t])
+
+        def coef_pass(c, t, g):
+            if g == 0:
+                coef_bank[c, t] = bank([P, CHUNK])
+            if c == 0:
+                zw, zs = z_first[:, g, :], zs_first[:, g, :]
+            else:
+                zw = z_rest[:, g, 2 * (c - 1) * CHUNK : 2 * c * CHUNK]
+                zs = zs_rest[:, g, (c - 1) * CHUNK : c * CHUNK]
+            nc.tensor.matmul_mx(
+                out=coef_bank[c, t][:],
+                lhsT=u_st[:, t, g, :].bitcast(FP4X4),
+                lhsT_scale=us_st[:, t, g, :],
+                rhs=zw.bitcast(FP4X4),
+                rhs_scale=zs,
+                start=(g == 0),
+                stop=(g == GROUPS - 1),
+            )
+
+        def coef_passes(c, t):
+            for g in range(GROUPS):
+                coef_pass(c, t, g)
+
+        def coef_out(c, t):
+            nc.scalar.activation(out=coef16[:, t, :], in_=coef_bank[c, t][:], func=COPY, scale=norms32[:, t : t + 1])
+
+        def coef_interleave(c):
+            coef_grouped[c] = grouped_tile()
+            nc.vector.tensor_copy(
+                out=coef_grouped[c][:].rearrange("p (n i t) -> p n t i", i=4, t=PACK),
+                in_=coef16[:].rearrange("p t (n i) -> p n t i", i=4),
+            )
+
+        def coef_quantize(c):
+            nc.vector.quantize_mx(out=coef_codes[c][:].bitcast(FP8X4), scales=coef_scales[c][:], in_=coef_grouped[c][:])
+
+        def ctl_transposes(g):
+            words = ctl_raw[g][:].bitcast(F32)
+            for h in range(2):
+                ctl_bank[g, h] = bank([P, 2, 2, P])
+                for a in range(2):
+                    for u in range(2):
+                        nc.tensor.transpose(ctl_bank[g, h][:, a, u, :], words[:, 2 * h + a, u : 2 * P : 2], ident[:])
+
+        def ctl_out(g):
+            ctl_grouped[g] = grouped_tile()
+            dst = ctl_grouped[g][:].bitcast(F32).rearrange("p (h a m u) -> p h a m u", h=2, a=2, u=2)
+            for h in range(2):
+                nc.scalar.copy(out=dst[:, h], in_=ctl_bank[g, h][:].rearrange("p a u m -> p a m u"))
+
+        def ctl_quantize(g):
+            nc.vector.quantize_mx(out=ctl_codes[g][:].bitcast(FP8X4), scales=ctl_scales[g][:], in_=ctl_grouped[g][:])
+
+        def weigh(i):
+            g, c = UNITS[i]
+            for t in range(PACK):
+                nc.gpsimd.tensor_scalar(
+                    out=y32[i][:, t, :], in0=trt[g, c][:, t, :], scalar1=w32[:, g, t : t + 1], scalar2=0.0,
+                    op0=ALU.mult, op1=ALU.add,
+                )
+
+        def fit(i, t):
+            g, c = UNITS[i]
+            fit_bank[i, t] = bank([P, CHUNK])
+            nc.tensor.matmul_mx(
+                out=fit_bank[i, t][:],
+                lhsT=ctl_codes[g][:, t * P : (t + 1) * P].bitcast(FP8X4),
+                lhsT_scale=ctl_scales[g][:, t * P : (t + 1) * P],
+                rhs=coef_codes[c][:].bitcast(FP8X4),
+                rhs_scale=coef_scales[c][:],
+                start=True,
+                stop=True,
+            )
+
+        def residual(i, t):
+            g = UNITS[i][0]
+            dst = y32[i][:, t, :]
+            nc.vector.scalar_tensor_tensor(
+                out=dst, in0=fit_bank[i, t][:], scalar=negw32[:, g, t : t + 1], in1=dst, op0=ALU.mult, op1=ALU.add
+            )
+
+        def unit(i, beside):
+            for t in range(PACK):
+                fit(i, t)
+                residual(i, t)
+                for step in beside[t::PACK] if len(beside) <= PACK else beside[2 * t : 2 * t + 2]:
+                    coef_pass(*step)
+
+        def y_interleave(i, h0=0, h1=2, copy=nc.scalar.copy):
+            if h0 == 0:
+                y_grouped[i] = grouped_tile()
+            half = CHUNK // 2
+            src = y32[i][:, :, h0 * half : h1 * half]
+            dst = y_grouped[i][:, h0 * half * PACK : h1 * half * PACK]
+            copy(
+                out=dst.rearrange("p (n i t) -> p n t i", i=2, t=PACK),
+                in_=src.rearrange("p t (n i) -> p n t i", i=2),
+            )
+
+        def y_quantize(i):
+            g, c = UNITS[i]
+            y_codes[i] = turn.tile([P, CHUNK], U32, name="y_codes", bufs=6, align_bytes=64)
+            nc.vector.quantize_mx(
+                out=y_codes[i][:].bitcast(FP8X4), scales=y_scales[4 * g : P, cols(c)], in_=y_grouped[i][:]
+            )
+
+        def store_y(i, t0=0, t1=PACK):
+            g, c = UNITS[i]
+            dst = out_0[rows(g), cols(c)].rearrange("(p t) m -> p t m", t=PACK)
+            nc.sync.dma_start(out=dst[:, t0:t1, :], in_=y32[i][:, t0:t1, :])
+
+        def store_codes(i):
+            g, c = UNITS[i]
+            dst = out_1[g].rearrange("p m t -> p (m t)").bitcast(I32)
+            nc.sync.dma_start(out=dst[:, cols(c)], in_=y_codes[i][:].bitcast(I32))
+
+        nc.vector.memset(us_raw[:].bitcast(I32), 0)
+        nc.vector.memset(zs_first[:].bitcast(I32), 0)
+        nc.vector.memset(zs_rest[:].bitcast(I32), 0)
+        make_identity(nc, ident[:])
+        load_words(u_raw, u_words, 0, 2 * N_CTL)
+        load_scale_rows(us_raw, u_scales, 0, N_CTL, range(4))
+        load_words(z_first, z_words, 0, 2 * CHUNK)
+        load_scale_rows(zs_first, z_scales, 0, CHUNK, range(4))
+        nc.sync.dma_start(out=norms16[:], in_=norms.rearrange("(p t) -> p t", t=PACK))
+        load_controls(0)
+        nc.sync.dma_start(out=w16[:], in_=row_weight.rearrange("(g p t) -> p g t", p=P, t=PACK))
+        load_treatments(0, 0, 1)
+        load_controls(1)
+        load_scale_rows(zs_rest, z_scales, CHUNK, N_TRT, range(4))
+        load_words(z_rest, z_words, 2 * CHUNK, 2 * N_TRT)
+        load_treatments(1, 0, 1)
+        load_treatments(0, 1, 3)
+        load_treatments(1, 1, 3)
+
+        nc.scalar.activation(out=norms32[:], in_=norms16[:], func=COPY)
+        for t in range(PACK):
+            order_u(t)
+            coef_passes(0, t)
+            coef_out(0, t)
+        nc.vector.tensor_copy(out=w32[:], in_=w16[:])
+        nc.vector.tensor_scalar(out=negw32[:], in0=w16[:], scalar1=-1.0, scalar2=None, op0=ALU.mult)
+        ctl_transposes(0)
+        ctl_out(0)
+        ctl_transposes(1)
+        ctl_out(1)
+        load_controls(2)
+        load_treatments(2, 0, 3)
+        load_controls(3)
+        load_treatments(3, 0, 3)
+        for i in range(len(UNITS)):
+            weigh(i)
+        coef_interleave(0)
+        ctl_quantize(0)
+        coef_quantize(0)
+        coef_passes(1, 0)
+        coef_out(1, 0)
+        unit(0, [(1, 1, g) for g in range(GROUPS)])
+        coef_out(1, 1)
+        ctl_quantize(1)
+        coef_pass(1, 2, 0)
+        coef_pass(1, 2, 1)
+        y_interleave(0, 0, 1)
+        unit(1, [(1, 2, 2), (1, 2, 3), (1, 3, 0), (1, 3, 1), (1, 3, 2), (1, 3, 3)])
+        coef_out(1, 2)
+        coef_out(1, 3)
+        y_interleave(0, 1, 2)
+        coef_interleave(1)
+        y_quantize(0)
+        coef_quantize(1)
+        y_interleave(1)
+        store_y(0)
+        store_y(1)
+        store_codes(0)
+        for t in range(3):
+            coef_passes(2, t)
+        unit(2, [(2, 3, g) for g in range(GROUPS)])
+        for t in range(PACK):
+            coef_out(2, t)
+        y_quantize(1)
+        store_codes(1)
+        store_y(2)
+        y_interleave(2)
+        unit(3, [])
+        ctl_transposes(2)
+        ctl_out(2)
+        store_y(3)
+        coef_interleave(2)
+        y_quantize(2)
+        coef_quantize(2)
+        ctl_quantize(2)
+        store_codes(2)
+        y_interleave(3)
+        last = len(UNITS) - 1
+        for i in range(4, last):
+            unit(i, [])
+            if i == 5:
+                ctl_transposes(3)
+                ctl_out(3)
+            y_quantize(i - 1)
+            if i == 6:
+                ctl_quantize(3)
+            store_y(i)
+            store_codes(i - 1)
+            y_interleave(i)
+        unit(last, [])
+        store_y(last, 0, 2)
+        store_y(last, 2, 4)
+        y_quantize(last - 1)
+        store_codes(last - 1)
+        y_interleave(last, 0, 1)
+        y_interleave(last, 1, 2, nc.vector.tensor_copy)
+        y_quantize(last)
+        store_codes(last)
+        for q in range(4):
+            nc.sync.dma_start(
+                out=out_2[:, 4 * q : 4 * q + 4, :].bitcast(I32), in_=y_scales[32 * q : 32 * q + 16, :].bitcast(I32)
+            )

@@ -22,7 +22,21 @@ GROUP = P * PACK
 GROUPS = N_OBS // GROUP
 CHUNK = 512
 CHUNKS = N_TRT // CHUNK
-UNITS = [(0, 0), (1, 0), (0, 1), (1, 1), (0, 2), (1, 2), (2, 0), (2, 1), (2, 2), (3, 0), (3, 1), (3, 2)]
+UNITS = [(0, 0), (1, 0), (0, 1), (1, 1), (2, 0), (2, 1), (0, 2), (1, 2), (2, 2), (3, 0), (3, 1), (3, 2)]
+Y_SLOTS = 8
+GP = {
+    1: [(3, 3), (3, 0)],
+    2: [(4, 3), (4, 0), (5, 0)],
+    3: [(5, 3), (5, 1), (5, 2)],
+    4: [(7, 3), (7, 0)],
+    5: [(8, 3), (7, 1)],
+    6: [(9, 3), (8, 0), (8, 1)],
+    7: [(10, 3), (8, 2), (9, 0)],
+    8: [(11, 3), (9, 1), (9, 2)],
+    9: [(10, 0), (10, 1), (10, 2)],
+    10: [(11, 0), (11, 1), (11, 2)],
+}
+WARM = 3
 
 
 def tile_frisch_waugh_partialling_k5_kernel(
@@ -41,9 +55,6 @@ def tile_frisch_waugh_partialling_k5_kernel(
         def bank(shape):
             return psum.tile(shape, F32, name="bank")
 
-        def grouped_tile():
-            return turn.tile([P, CHUNK * PACK], BF16, name="grouped", bufs=4, align_bytes=64)
-
         def cols(c):
             return slice(c * CHUNK, (c + 1) * CHUNK)
 
@@ -58,9 +69,8 @@ def tile_frisch_waugh_partialling_k5_kernel(
         zs_first = kept("zs_first", [P, GROUPS, CHUNK], U8)
         z_rest = kept("z_rest", [P, GROUPS, 2 * (N_TRT - CHUNK)], U8)
         zs_rest = kept("zs_rest", [P, GROUPS, N_TRT - CHUNK], U8)
-        norms16 = kept("norms16", [P, PACK], BF16)
+        vectors = kept("vectors", [P, GROUP], BF16)
         norms32 = kept("norms32", [P, PACK], F32)
-        w16 = kept("w16", [P, GROUPS, PACK], BF16)
         w32 = kept("w32", [P, GROUPS, PACK], F32)
         negw32 = kept("negw32", [P, GROUPS, PACK], F32)
         ident = kept("ident", [P, P], F32)
@@ -69,25 +79,31 @@ def tile_frisch_waugh_partialling_k5_kernel(
         coef_scales = [kept("coef_scales%d" % c, [P, CHUNK], U8) for c in range(CHUNKS)]
         ctl_codes = [kept("ctl_codes%d" % g, [P, GROUP], U32) for g in range(GROUPS)]
         ctl_scales = [kept("ctl_scales%d" % g, [P, GROUP], U8) for g in range(GROUPS)]
-        y32 = [kept("y32_%d" % i, [P, PACK, CHUNK], F32) for i in range(len(UNITS))]
+        y_slots = [kept("y32_%d" % i, [P, PACK, CHUNK], F32) for i in range(Y_SLOTS)]
+        y32 = [y_slots[i % Y_SLOTS] for i in range(len(UNITS))]
+        side = {(i, 3): kept("side%d" % i, [P, CHUNK], F32)[:] for i in (0, 1, 2, 6)}
+        y_codes = [kept("y_codes%d" % g, [P, N_TRT], U32) for g in range(GROUPS)]
         y_scales = kept("y_scales", [P, N_TRT], U8)
         trt = {}
         ctl_raw = {}
         coef_bank = {}
         ctl_bank = {}
         fit_bank = {}
-        ctl_grouped = {}
-        coef_grouped = {}
-        y_grouped = {}
-        y_codes = {}
+        ctl_pair = [kept("ctl_grouped%d" % n, [P, GROUP * PACK], BF16) for n in range(2)]
+        ctl_grouped = [ctl_pair[g % 2] for g in range(GROUPS)]
+        coef_one = kept("coef_grouped", [P, CHUNK * PACK], BF16)
+        coef_grouped = [coef_one] * CHUNKS
+        y_ring = [kept("y_grouped%d" % n, [P, CHUNK * PACK], BF16) for n in range(3)]
+        y_grouped = [y_ring[i % 3] for i in range(len(UNITS))]
 
-        def load_scale_rows(plane, src, c0, c1, rs):
+        def load_scale_rows(queue, plane, src, c0, c1, rs=range(4)):
             view = src.rearrange("g (q r) n -> r q g n", r=4)
             for r in rs:
-                nc.sync.dma_start(out=plane[r:P:32].bitcast(I32), in_=view[r][:, :, c0:c1].bitcast(I32))
+                queue.dma_start(out=plane[r:P:32].bitcast(I32), in_=view[r][:, :, c0:c1].bitcast(I32))
 
-        def load_words(dst, src, b0, b1):
-            nc.sync.dma_start(out=dst[:].bitcast(I32), in_=src.rearrange("g p b -> p g b")[:, :, b0:b1].bitcast(I32))
+        def load_words(dst, src, b0, b1, g0=0, g1=GROUPS):
+            view = src.rearrange("g p b -> p g b")[:, g0:g1, b0:b1]
+            nc.sync.dma_start(out=dst[:, g0:g1, :].bitcast(I32), in_=view.bitcast(I32))
 
         def load_controls(g):
             ctl_raw[g] = turn.tile([P, PACK, N_CTL], BF16, name="ctl_raw", align_bytes=64)
@@ -133,7 +149,6 @@ def tile_frisch_waugh_partialling_k5_kernel(
             nc.scalar.activation(out=coef16[:, t, :], in_=coef_bank[c, t][:], func=COPY, scale=norms32[:, t : t + 1])
 
         def coef_interleave(c):
-            coef_grouped[c] = grouped_tile()
             nc.vector.tensor_copy(
                 out=coef_grouped[c][:].rearrange("p (n i t) -> p n t i", i=4, t=PACK),
                 in_=coef16[:].rearrange("p t (n i) -> p n t i", i=4),
@@ -142,30 +157,42 @@ def tile_frisch_waugh_partialling_k5_kernel(
         def coef_quantize(c):
             nc.vector.quantize_mx(out=coef_codes[c][:].bitcast(FP8X4), scales=coef_scales[c][:], in_=coef_grouped[c][:])
 
-        def ctl_transposes(g):
+        def ctl_transposes(g, hs=(0, 1)):
             words = ctl_raw[g][:].bitcast(F32)
-            for h in range(2):
+            for h in hs:
                 ctl_bank[g, h] = bank([P, 2, 2, P])
                 for a in range(2):
                     for u in range(2):
                         nc.tensor.transpose(ctl_bank[g, h][:, a, u, :], words[:, 2 * h + a, u : 2 * P : 2], ident[:])
 
-        def ctl_out(g):
-            ctl_grouped[g] = grouped_tile()
+        def ctl_out(g, hs=(0, 1)):
             dst = ctl_grouped[g][:].bitcast(F32).rearrange("p (h a m u) -> p h a m u", h=2, a=2, u=2)
-            for h in range(2):
+            for h in hs:
                 nc.scalar.copy(out=dst[:, h], in_=ctl_bank[g, h][:].rearrange("p a u m -> p a m u"))
 
         def ctl_quantize(g):
             nc.vector.quantize_mx(out=ctl_codes[g][:].bitcast(FP8X4), scales=ctl_scales[g][:], in_=ctl_grouped[g][:])
 
-        def weigh(i):
+        def weighed(i, t):
+            return side.get((i, t), y32[i][:, t, :])
+
+        def weigh(engine, i, t):
             g, c = UNITS[i]
-            for t in range(PACK):
-                nc.gpsimd.tensor_scalar(
-                    out=y32[i][:, t, :], in0=trt[g, c][:, t, :], scalar1=w32[:, g, t : t + 1], scalar2=0.0,
-                    op0=ALU.mult, op1=ALU.add,
-                )
+            engine.tensor_scalar(
+                out=weighed(i, t), in0=trt[g, c][:, t, :], scalar1=w32[:, g, t : t + 1], scalar2=0.0,
+                op0=ALU.mult, op1=ALU.add,
+            )
+
+        def weigh_scalar(i, t):
+            g, c = UNITS[i]
+            nc.scalar.activation(out=weighed(i, t), in_=trt[g, c][:, t, :], func=COPY, scale=w32[:, g, t : t + 1])
+
+        def weigh_beside(j):
+            steps = GP.get(j, [])
+            if steps:
+                side[steps[0]] = side[j - 1, 3]
+            for i, t in steps:
+                weigh(nc.gpsimd, i, t)
 
         def fit(i, t):
             g, c = UNITS[i]
@@ -182,21 +209,21 @@ def tile_frisch_waugh_partialling_k5_kernel(
 
         def residual(i, t):
             g = UNITS[i][0]
-            dst = y32[i][:, t, :]
             nc.vector.scalar_tensor_tensor(
-                out=dst, in0=fit_bank[i, t][:], scalar=negw32[:, g, t : t + 1], in1=dst, op0=ALU.mult, op1=ALU.add
+                out=y32[i][:, t, :], in0=fit_bank[i, t][:], scalar=negw32[:, g, t : t + 1], in1=weighed(i, t),
+                op0=ALU.mult, op1=ALU.add,
             )
 
-        def unit(i, beside):
-            for t in range(PACK):
+        def unit(i, beside, t0=0, t1=PACK):
+            if t0 == 0:
+                weigh_beside(i)
+            for t in range(t0, t1):
                 fit(i, t)
                 residual(i, t)
-                for step in beside[t::PACK] if len(beside) <= PACK else beside[2 * t : 2 * t + 2]:
+                for step in beside[t - t0]:
                     coef_pass(*step)
 
         def y_interleave(i, h0=0, h1=2, copy=nc.scalar.copy):
-            if h0 == 0:
-                y_grouped[i] = grouped_tile()
             half = CHUNK // 2
             src = y32[i][:, :, h0 * half : h1 * half]
             dst = y_grouped[i][:, h0 * half * PACK : h1 * half * PACK]
@@ -207,9 +234,8 @@ def tile_frisch_waugh_partialling_k5_kernel(
 
         def y_quantize(i):
             g, c = UNITS[i]
-            y_codes[i] = turn.tile([P, CHUNK], U32, name="y_codes", bufs=6, align_bytes=64)
             nc.vector.quantize_mx(
-                out=y_codes[i][:].bitcast(FP8X4), scales=y_scales[4 * g : P, cols(c)], in_=y_grouped[i][:]
+                out=y_codes[g][:, cols(c)].bitcast(FP8X4), scales=y_scales[4 * g : P, cols(c)], in_=y_grouped[i][:]
             )
 
         def store_y(i, t0=0, t1=PACK):
@@ -220,98 +246,136 @@ def tile_frisch_waugh_partialling_k5_kernel(
         def store_codes(i):
             g, c = UNITS[i]
             dst = out_1[g].rearrange("p m t -> p (m t)").bitcast(I32)
-            nc.sync.dma_start(out=dst[:, cols(c)], in_=y_codes[i][:].bitcast(I32))
+            nc.sync.dma_start(out=dst[:, cols(c)], in_=y_codes[g][:, cols(c)].bitcast(I32))
 
-        nc.vector.memset(us_raw[:].bitcast(I32), 0)
+        nc.vector.memset(vectors[:].bitcast(I32), 0)
         nc.vector.memset(zs_first[:].bitcast(I32), 0)
+        nc.vector.memset(us_raw[:].bitcast(I32), 0)
         nc.vector.memset(zs_rest[:].bitcast(I32), 0)
+        load_scale_rows(nc.gpsimd, zs_first, z_scales, 0, CHUNK, (2, 3))
         make_identity(nc, ident[:])
+        load_scale_rows(nc.gpsimd, zs_rest, z_scales, CHUNK, N_TRT)
         load_words(u_raw, u_words, 0, 2 * N_CTL)
-        load_scale_rows(us_raw, u_scales, 0, N_CTL, range(4))
+        nc.sync.dma_start(out=vectors[0:GROUPS, :], in_=row_weight.rearrange("(g k) -> g k", g=GROUPS))
+        nc.sync.dma_start(out=vectors[GROUPS : GROUPS + 1, :], in_=norms.rearrange("(o k) -> o k", o=1))
+        load_scale_rows(nc.sync, us_raw, u_scales, 0, N_CTL)
         load_words(z_first, z_words, 0, 2 * CHUNK)
-        load_scale_rows(zs_first, z_scales, 0, CHUNK, range(4))
-        nc.sync.dma_start(out=norms16[:], in_=norms.rearrange("(p t) -> p t", t=PACK))
+        load_scale_rows(nc.sync, zs_first, z_scales, 0, CHUNK, (0, 1))
+        load_treatments(0, 0, 3)
         load_controls(0)
-        nc.sync.dma_start(out=w16[:], in_=row_weight.rearrange("(g p t) -> p g t", p=P, t=PACK))
-        load_treatments(0, 0, 1)
+        load_words(z_rest, z_words, 2 * CHUNK, 2 * N_TRT, 0, 2)
         load_controls(1)
-        load_scale_rows(zs_rest, z_scales, CHUNK, N_TRT, range(4))
-        load_words(z_rest, z_words, 2 * CHUNK, 2 * N_TRT)
+        load_words(z_rest, z_words, 2 * CHUNK, 2 * N_TRT, 2, 4)
         load_treatments(1, 0, 1)
-        load_treatments(0, 1, 3)
         load_treatments(1, 1, 3)
+        load_treatments(2, 0, 3)
 
-        nc.scalar.activation(out=norms32[:], in_=norms16[:], func=COPY)
+        none = [[]] * PACK
+        vec_bank = bank([P, 2, P])
+        for u in range(2):
+            nc.tensor.transpose(vec_bank[:, u, :], vectors[:].bitcast(F32)[:, u : 2 * P : 2], ident[:])
+        turned = vec_bank[:].bitcast(BF16).rearrange("p u (j e) -> p j u e", e=2)
+        nc.scalar.activation(out=norms32[:].rearrange("p (u e) -> p u e", e=2), in_=turned[:, GROUPS], func=COPY)
+        nc.scalar.activation(out=w32[:].rearrange("p g (u e) -> p g u e", e=2), in_=turned[:, :GROUPS], func=COPY)
+        nc.scalar.activation(
+            out=negw32[:].rearrange("p g (u e) -> p g u e", e=2), in_=turned[:, :GROUPS], func=COPY, scale=-1.0
+        )
+        warm_bank = bank([P, CHUNK])
+        for n in range(WARM):
+            nc.tensor.matmul_mx(
+                out=warm_bank[:],
+                lhsT=u_raw[:, 0, : 2 * P].bitcast(FP4X4),
+                lhsT_scale=us_raw[:, 0, :P],
+                rhs=u_raw[:, 0, :].bitcast(FP4X4),
+                rhs_scale=us_raw[:, 0, :],
+                start=True,
+                stop=True,
+            )
         for t in range(PACK):
             order_u(t)
+        for i in (0, 2, 6):
+            for t in range(PACK):
+                weigh(nc.vector, i, t)
+        for t in range(PACK):
             coef_passes(0, t)
             coef_out(0, t)
-        nc.vector.tensor_copy(out=w32[:], in_=w16[:])
-        nc.vector.tensor_scalar(out=negw32[:], in0=w16[:], scalar1=-1.0, scalar2=None, op0=ALU.mult)
         ctl_transposes(0)
         ctl_out(0)
+        load_controls(2)
         ctl_transposes(1)
         ctl_out(1)
-        load_controls(2)
-        load_treatments(2, 0, 3)
         load_controls(3)
-        load_treatments(3, 0, 3)
-        for i in range(len(UNITS)):
-            weigh(i)
         coef_interleave(0)
         ctl_quantize(0)
         coef_quantize(0)
+        ctl_quantize(1)
         coef_passes(1, 0)
         coef_out(1, 0)
-        unit(0, [(1, 1, g) for g in range(GROUPS)])
+        for t in range(PACK):
+            unit(0, [[(1, 1 + t // 2, 2 * (t % 2)), (1, 1 + t // 2, 2 * (t % 2) + 1)]], t, t + 1)
+            weigh(nc.vector, 1, t)
+        weigh_scalar(3, 1)
         coef_out(1, 1)
-        ctl_quantize(1)
-        coef_pass(1, 2, 0)
-        coef_pass(1, 2, 1)
-        y_interleave(0, 0, 1)
-        unit(1, [(1, 2, 2), (1, 2, 3), (1, 3, 0), (1, 3, 1), (1, 3, 2), (1, 3, 3)])
+        weigh_scalar(3, 2)
         coef_out(1, 2)
+        y_interleave(0, 0, 1)
+        unit(1, [[(1, 3, g) for g in range(GROUPS)], [], []], 0, 3)
         coef_out(1, 3)
         y_interleave(0, 1, 2)
         coef_interleave(1)
-        y_quantize(0)
+        unit(1, none, 3, 4)
         coef_quantize(1)
-        y_interleave(1)
-        store_y(0)
-        store_y(1)
-        store_codes(0)
-        for t in range(3):
-            coef_passes(2, t)
-        unit(2, [(2, 3, g) for g in range(GROUPS)])
-        for t in range(PACK):
-            coef_out(2, t)
-        y_quantize(1)
-        store_codes(1)
-        store_y(2)
-        y_interleave(2)
-        unit(3, [])
+        coef_passes(2, 0)
         ctl_transposes(2)
         ctl_out(2)
-        store_y(3)
-        coef_interleave(2)
-        y_quantize(2)
-        coef_quantize(2)
+        y_interleave(1)
+        weigh_scalar(4, 1)
+        weigh_scalar(4, 2)
+        coef_out(2, 0)
+        store_y(0)
+        store_y(1)
+        load_treatments(3, 0, 3)
+        unit(2, none, 0, 3)
+        y_quantize(0)
         ctl_quantize(2)
+        unit(2, [[(2, 1, g) for g in range(GROUPS)]], 3, 4)
+        y_quantize(1)
+        y_interleave(2)
+        coef_out(2, 1)
+        store_codes(0)
+        store_y(2)
+        store_codes(1)
+        unit(3, [[], [], [], [(2, t, g) for t in (2, 3) for g in range(GROUPS)]])
+        y_quantize(2)
+        coef_out(2, 2)
+        coef_out(2, 3)
+        store_y(3)
         store_codes(2)
         y_interleave(3)
+        unit(4, none, 0, 3)
+        ctl_transposes(3)
+        ctl_out(3)
+        coef_interleave(2)
+        y_quantize(3)
+        unit(4, none, 3, 4)
+        coef_quantize(2)
+        store_codes(3)
+        store_y(4)
+        y_interleave(4)
+        weigh_scalar(7, 2)
         last = len(UNITS) - 1
-        for i in range(4, last):
-            unit(i, [])
+        for i in range(5, last):
             if i == 5:
-                ctl_transposes(3)
-                ctl_out(3)
-            y_quantize(i - 1)
-            if i == 6:
+                unit(i, none, 0, 3)
                 ctl_quantize(3)
+                unit(i, none, 3, 4)
+            else:
+                unit(i, none)
+            y_quantize(i - 1)
             store_y(i)
             store_codes(i - 1)
             y_interleave(i)
-        unit(last, [])
+        unit(last, none)
         store_y(last, 0, 2)
         store_y(last, 2, 4)
         y_quantize(last - 1)

@@ -28,15 +28,16 @@ GP = {
     1: [(3, 3), (3, 0)],
     2: [(4, 3), (4, 0), (5, 0)],
     3: [(5, 3), (5, 1), (5, 2)],
-    4: [(7, 3), (7, 0)],
-    5: [(8, 3), (7, 1)],
-    6: [(9, 3), (8, 0), (8, 1)],
-    7: [(10, 3), (8, 2), (9, 0)],
-    8: [(11, 3), (9, 1), (9, 2)],
-    9: [(10, 0), (10, 1), (10, 2)],
+    4: [(6, 3), (6, 0)],
+    5: [(7, 3), (6, 1)],
+    6: [(8, 3), (7, 0), (7, 1)],
+    7: [(9, 3), (8, 0), (8, 1)],
+    8: [(10, 3), (9, 0), (9, 1)],
+    9: [(11, 3), (10, 0), (10, 1)],
     10: [(11, 0), (11, 1), (11, 2)],
 }
 WARM = 3
+SPLIT = 3
 
 
 def tile_frisch_waugh_partialling_k5_kernel(
@@ -81,7 +82,7 @@ def tile_frisch_waugh_partialling_k5_kernel(
         ctl_scales = [kept("ctl_scales%d" % g, [P, GROUP], U8) for g in range(GROUPS)]
         y_slots = [kept("y32_%d" % i, [P, PACK, CHUNK], F32) for i in range(Y_SLOTS)]
         y32 = [y_slots[i % Y_SLOTS] for i in range(len(UNITS))]
-        side = {(i, 3): kept("side%d" % i, [P, CHUNK], F32)[:] for i in (0, 1, 2, 6)}
+        side = {(i, 3): kept("side%d" % i, [P, CHUNK], F32)[:] for i in range(3)}
         y_codes = [kept("y_codes%d" % g, [P, N_TRT], U32) for g in range(GROUPS)]
         y_scales = kept("y_scales", [P, N_TRT], U8)
         trt = {}
@@ -109,12 +110,14 @@ def tile_frisch_waugh_partialling_k5_kernel(
             ctl_raw[g] = turn.tile([P, PACK, N_CTL], BF16, name="ctl_raw", align_bytes=64)
             nc.sync.dma_start(out=ctl_raw[g][:], in_=controls[rows(g), :].rearrange("(m t) k -> m t k", t=PACK))
 
-        def load_treatments(g, c0, c1):
+        def load_treatments(g, c0, c1, halves=1):
             tile = kept("trt_%d_%d" % (g, c0), [P, PACK, (c1 - c0) * CHUNK], BF16)
             for c in range(c0, c1):
                 trt[g, c] = tile[:, :, (c - c0) * CHUNK : (c - c0 + 1) * CHUNK]
-            src = treatments[rows(g), c0 * CHUNK : c1 * CHUNK]
-            nc.sync.dma_start(out=tile[:], in_=src.rearrange("(p t) m -> p t m", t=PACK))
+            src = treatments[rows(g), c0 * CHUNK : c1 * CHUNK].rearrange("(p t) m -> p t m", t=PACK)
+            step = PACK // halves
+            for t0 in range(0, PACK, step):
+                nc.sync.dma_start(out=tile[:, t0 : t0 + step, :], in_=src[:, t0 : t0 + step, :])
 
         def order_u(t):
             nc.vector.tensor_copy(
@@ -223,8 +226,8 @@ def tile_frisch_waugh_partialling_k5_kernel(
                 for step in beside[t - t0]:
                     coef_pass(*step)
 
-        def y_interleave(i, h0=0, h1=2, copy=nc.scalar.copy):
-            half = CHUNK // 2
+        def y_interleave(i, h0=0, h1=8, copy=nc.scalar.copy):
+            half = CHUNK // 8
             src = y32[i][:, :, h0 * half : h1 * half]
             dst = y_grouped[i][:, h0 * half * PACK : h1 * half * PACK]
             copy(
@@ -252,20 +255,19 @@ def tile_frisch_waugh_partialling_k5_kernel(
         nc.vector.memset(zs_first[:].bitcast(I32), 0)
         nc.vector.memset(us_raw[:].bitcast(I32), 0)
         nc.vector.memset(zs_rest[:].bitcast(I32), 0)
-        load_scale_rows(nc.gpsimd, zs_first, z_scales, 0, CHUNK, (2, 3))
         make_identity(nc, ident[:])
-        load_scale_rows(nc.gpsimd, zs_rest, z_scales, CHUNK, N_TRT)
         load_words(u_raw, u_words, 0, 2 * N_CTL)
         nc.sync.dma_start(out=vectors[0:GROUPS, :], in_=row_weight.rearrange("(g k) -> g k", g=GROUPS))
         nc.sync.dma_start(out=vectors[GROUPS : GROUPS + 1, :], in_=norms.rearrange("(o k) -> o k", o=1))
         load_scale_rows(nc.sync, us_raw, u_scales, 0, N_CTL)
         load_words(z_first, z_words, 0, 2 * CHUNK)
-        load_scale_rows(nc.sync, zs_first, z_scales, 0, CHUNK, (0, 1))
-        load_treatments(0, 0, 3)
+        load_scale_rows(nc.sync, zs_first, z_scales, 0, CHUNK)
+        load_treatments(0, 0, 2, 2)
         load_controls(0)
+        load_scale_rows(nc.sync, zs_rest, z_scales, CHUNK, N_TRT)
         load_words(z_rest, z_words, 2 * CHUNK, 2 * N_TRT, 0, 2)
-        load_controls(1)
         load_words(z_rest, z_words, 2 * CHUNK, 2 * N_TRT, 2, 4)
+        load_controls(1)
         load_treatments(1, 0, 1)
         load_treatments(1, 1, 3)
         load_treatments(2, 0, 3)
@@ -293,8 +295,8 @@ def tile_frisch_waugh_partialling_k5_kernel(
             )
         for t in range(PACK):
             order_u(t)
-        for i in (0, 2, 6):
-            for t in range(PACK):
+        for t in range(PACK):
+            for i in (0, 2):
                 weigh(nc.vector, i, t)
         for t in range(PACK):
             coef_passes(0, t)
@@ -302,67 +304,74 @@ def tile_frisch_waugh_partialling_k5_kernel(
         ctl_transposes(0)
         ctl_out(0)
         load_controls(2)
-        ctl_transposes(1)
-        ctl_out(1)
-        load_controls(3)
         coef_interleave(0)
         ctl_quantize(0)
         coef_quantize(0)
+        for t in range(2):
+            coef_pass(1, t, 0)
+            coef_pass(1, t, 1)
+        for t in range(2):
+            coef_pass(1, t, 2)
+            coef_pass(1, t, 3)
+            coef_out(1, t)
+        unit(0, none, 0, 2)
+        weigh(nc.vector, 1, 2)
+        weigh(nc.vector, 1, 3)
+        unit(0, none, 2, 4)
+        ctl_transposes(1)
+        weigh_scalar(1, 0)
+        ctl_out(1)
+        weigh_scalar(1, 1)
         ctl_quantize(1)
-        coef_passes(1, 0)
-        coef_out(1, 0)
-        for t in range(PACK):
-            unit(0, [[(1, 1 + t // 2, 2 * (t % 2)), (1, 1 + t // 2, 2 * (t % 2) + 1)]], t, t + 1)
-            weigh(nc.vector, 1, t)
-        weigh_scalar(3, 1)
-        coef_out(1, 1)
-        weigh_scalar(3, 2)
-        coef_out(1, 2)
-        y_interleave(0, 0, 1)
-        unit(1, [[(1, 3, g) for g in range(GROUPS)], [], []], 0, 3)
-        coef_out(1, 3)
-        y_interleave(0, 1, 2)
+        for t in (2, 3):
+            coef_passes(1, t)
+            coef_out(1, t)
+        y_interleave(0)
+        unit(1, none, 0, 2)
         coef_interleave(1)
-        unit(1, none, 3, 4)
+        unit(1, none, 2, 3)
         coef_quantize(1)
+        unit(1, none, 3, 4)
         coef_passes(2, 0)
+        coef_out(2, 0)
+        weigh_scalar(3, 1)
+        weigh_scalar(3, 2)
         ctl_transposes(2)
         ctl_out(2)
         y_interleave(1)
         weigh_scalar(4, 1)
         weigh_scalar(4, 2)
-        coef_out(2, 0)
         store_y(0)
+        load_treatments(0, 2, 3)
         store_y(1)
-        load_treatments(3, 0, 3)
+        load_controls(3)
         unit(2, none, 0, 3)
-        y_quantize(0)
         ctl_quantize(2)
-        unit(2, [[(2, 1, g) for g in range(GROUPS)]], 3, 4)
-        y_quantize(1)
-        y_interleave(2)
+        unit(2, [[(2, t, g) for t in (1, 2) for g in range(GROUPS)]], 3, 4)
+        y_quantize(0)
         coef_out(2, 1)
-        store_codes(0)
-        store_y(2)
-        store_codes(1)
-        unit(3, [[], [], [], [(2, t, g) for t in (2, 3) for g in range(GROUPS)]])
-        y_quantize(2)
         coef_out(2, 2)
+        y_interleave(2)
+        store_y(2)
+        store_codes(0)
+        unit(3, [[], [], [], [(2, 3, g) for g in range(GROUPS)]])
+        y_quantize(1)
         coef_out(2, 3)
         store_y(3)
-        store_codes(2)
+        store_codes(1)
+        load_treatments(3, 0, 3)
         y_interleave(3)
         unit(4, none, 0, 3)
         ctl_transposes(3)
         ctl_out(3)
         coef_interleave(2)
-        y_quantize(3)
+        y_quantize(2)
         unit(4, none, 3, 4)
         coef_quantize(2)
-        store_codes(3)
+        store_codes(2)
         store_y(4)
         y_interleave(4)
-        weigh_scalar(7, 2)
+        weigh_scalar(6, 2)
         last = len(UNITS) - 1
         for i in range(5, last):
             if i == 5:
@@ -371,17 +380,21 @@ def tile_frisch_waugh_partialling_k5_kernel(
                 unit(i, none, 3, 4)
             else:
                 unit(i, none)
-            y_quantize(i - 1)
+            y_quantize(i - 2)
             store_y(i)
-            store_codes(i - 1)
+            store_codes(i - 2)
+            if i < last - 2:
+                weigh_scalar(i + 2, 2)
             y_interleave(i)
         unit(last, none)
         store_y(last, 0, 2)
         store_y(last, 2, 4)
+        y_quantize(last - 2)
+        store_codes(last - 2)
+        y_interleave(last, 0, SPLIT)
+        y_interleave(last, SPLIT, 8, nc.vector.tensor_copy)
         y_quantize(last - 1)
         store_codes(last - 1)
-        y_interleave(last, 0, 1)
-        y_interleave(last, 1, 2, nc.vector.tensor_copy)
         y_quantize(last)
         store_codes(last)
         for q in range(4):

@@ -25,17 +25,17 @@ CHUNKS = N_TRT // CHUNK
 UNITS = [(0, 0), (1, 0), (0, 1), (1, 1), (2, 0), (2, 1), (0, 2), (1, 2), (2, 2), (3, 0), (3, 1), (3, 2)]
 Y_SLOTS = 8
 GP = {
-    1: [(3, 3), (3, 0)],
     2: [(4, 3), (4, 0), (5, 0)],
     3: [(5, 3), (5, 1), (5, 2)],
-    4: [(6, 3), (6, 0)],
-    5: [(7, 3), (6, 1)],
-    6: [(8, 3), (7, 0), (7, 1)],
-    7: [(9, 3), (8, 0), (8, 1)],
-    8: [(10, 3), (9, 0), (9, 1)],
-    9: [(11, 3), (10, 0), (10, 1)],
+    4: [(7, 3), (7, 0)],
+    5: [(8, 3), (7, 1)],
+    6: [(9, 3), (8, 0), (8, 1)],
+    7: [(10, 3), (8, 2), (9, 0)],
+    8: [(11, 3), (9, 1), (9, 2)],
+    9: [(10, 0), (10, 1), (10, 2)],
     10: [(11, 0), (11, 1), (11, 2)],
 }
+CODES = {0: 0, 1: 0, 2: 1, 3: 1, 5: 0, 6: 2, 7: 2, 8: 2, 10: 0, 11: 2}
 WARM = 3
 SPLIT = 3
 
@@ -82,10 +82,10 @@ def tile_frisch_waugh_partialling_k5_kernel(
         ctl_scales = [kept("ctl_scales%d" % g, [P, GROUP], U8) for g in range(GROUPS)]
         y_slots = [kept("y32_%d" % i, [P, PACK, CHUNK], F32) for i in range(Y_SLOTS)]
         y32 = [y_slots[i % Y_SLOTS] for i in range(len(UNITS))]
-        side = {(i, 3): kept("side%d" % i, [P, CHUNK], F32)[:] for i in range(3)}
+        side = {(i, 3): kept("side%d" % i, [P, CHUNK], F32)[:] for i in (1, 2, 3, 6)}
         y_codes = [kept("y_codes%d" % g, [P, N_TRT], U32) for g in range(GROUPS)]
         y_scales = kept("y_scales", [P, N_TRT], U8)
-        trt = {}
+        trt = [kept("trt%d" % g, [P, PACK, N_TRT], BF16) for g in range(GROUPS)]
         ctl_raw = {}
         coef_bank = {}
         ctl_bank = {}
@@ -110,14 +110,9 @@ def tile_frisch_waugh_partialling_k5_kernel(
             ctl_raw[g] = turn.tile([P, PACK, N_CTL], BF16, name="ctl_raw", align_bytes=64)
             nc.sync.dma_start(out=ctl_raw[g][:], in_=controls[rows(g), :].rearrange("(m t) k -> m t k", t=PACK))
 
-        def load_treatments(g, c0, c1, halves=1):
-            tile = kept("trt_%d_%d" % (g, c0), [P, PACK, (c1 - c0) * CHUNK], BF16)
-            for c in range(c0, c1):
-                trt[g, c] = tile[:, :, (c - c0) * CHUNK : (c - c0 + 1) * CHUNK]
-            src = treatments[rows(g), c0 * CHUNK : c1 * CHUNK].rearrange("(p t) m -> p t m", t=PACK)
-            step = PACK // halves
-            for t0 in range(0, PACK, step):
-                nc.sync.dma_start(out=tile[:, t0 : t0 + step, :], in_=src[:, t0 : t0 + step, :])
+        def load_treatments(g, t0=0, t1=PACK):
+            src = treatments[rows(g), :].rearrange("(p t) m -> p t m", t=PACK)
+            nc.sync.dma_start(out=trt[g][:, t0:t1, :], in_=src[:, t0:t1, :])
 
         def order_u(t):
             nc.vector.tensor_copy(
@@ -182,13 +177,13 @@ def tile_frisch_waugh_partialling_k5_kernel(
         def weigh(engine, i, t):
             g, c = UNITS[i]
             engine.tensor_scalar(
-                out=weighed(i, t), in0=trt[g, c][:, t, :], scalar1=w32[:, g, t : t + 1], scalar2=0.0,
+                out=weighed(i, t), in0=trt[g][:, t, cols(c)], scalar1=w32[:, g, t : t + 1], scalar2=0.0,
                 op0=ALU.mult, op1=ALU.add,
             )
 
         def weigh_scalar(i, t):
             g, c = UNITS[i]
-            nc.scalar.activation(out=weighed(i, t), in_=trt[g, c][:, t, :], func=COPY, scale=w32[:, g, t : t + 1])
+            nc.scalar.activation(out=weighed(i, t), in_=trt[g][:, t, cols(c)], func=COPY, scale=w32[:, g, t : t + 1])
 
         def weigh_beside(j):
             steps = GP.get(j, [])
@@ -247,9 +242,12 @@ def tile_frisch_waugh_partialling_k5_kernel(
             nc.sync.dma_start(out=dst[:, t0:t1, :], in_=y32[i][:, t0:t1, :])
 
         def store_codes(i):
+            if i not in CODES:
+                return
             g, c = UNITS[i]
             dst = out_1[g].rearrange("p m t -> p (m t)").bitcast(I32)
-            nc.sync.dma_start(out=dst[:, cols(c)], in_=y_codes[g][:, cols(c)].bitcast(I32))
+            span = slice(CODES[i] * CHUNK, (c + 1) * CHUNK)
+            nc.sync.dma_start(out=dst[:, span], in_=y_codes[g][:, span].bitcast(I32))
 
         nc.vector.memset(vectors[:].bitcast(I32), 0)
         nc.vector.memset(zs_first[:].bitcast(I32), 0)
@@ -262,15 +260,15 @@ def tile_frisch_waugh_partialling_k5_kernel(
         load_scale_rows(nc.sync, us_raw, u_scales, 0, N_CTL)
         load_words(z_first, z_words, 0, 2 * CHUNK)
         load_scale_rows(nc.sync, zs_first, z_scales, 0, CHUNK)
-        load_treatments(0, 0, 2, 2)
+        load_treatments(0, 0, 2)
         load_controls(0)
         load_scale_rows(nc.sync, zs_rest, z_scales, CHUNK, N_TRT)
         load_words(z_rest, z_words, 2 * CHUNK, 2 * N_TRT, 0, 2)
         load_words(z_rest, z_words, 2 * CHUNK, 2 * N_TRT, 2, 4)
+        load_treatments(0, 2, 4)
         load_controls(1)
-        load_treatments(1, 0, 1)
-        load_treatments(1, 1, 3)
-        load_treatments(2, 0, 3)
+        load_treatments(1, 0, 2)
+        load_treatments(1, 2, 4)
 
         none = [[]] * PACK
         vec_bank = bank([P, 2, P])
@@ -295,8 +293,8 @@ def tile_frisch_waugh_partialling_k5_kernel(
             )
         for t in range(PACK):
             order_u(t)
-        for t in range(PACK):
-            for i in (0, 2):
+        for t in range(2):
+            for i in (0, 2, 6):
                 weigh(nc.vector, i, t)
         for t in range(PACK):
             coef_passes(0, t)
@@ -304,9 +302,12 @@ def tile_frisch_waugh_partialling_k5_kernel(
         ctl_transposes(0)
         ctl_out(0)
         load_controls(2)
+        load_treatments(2)
         coef_interleave(0)
         ctl_quantize(0)
         coef_quantize(0)
+        weigh(nc.vector, 0, 2)
+        weigh(nc.vector, 0, 3)
         for t in range(2):
             coef_pass(1, t, 0)
             coef_pass(1, t, 1)
@@ -314,18 +315,21 @@ def tile_frisch_waugh_partialling_k5_kernel(
             coef_pass(1, t, 2)
             coef_pass(1, t, 3)
             coef_out(1, t)
-        unit(0, none, 0, 2)
+        for t in range(PACK):
+            unit(0, [[(1, 2, t)]], t, t + 1)
+            weigh(nc.vector, (2, 6)[t % 2], 2 + t // 2)
+        coef_out(1, 2)
+        ctl_transposes(1)
+        ctl_out(1)
+        weigh(nc.vector, 1, 0)
+        weigh(nc.vector, 1, 1)
+        ctl_quantize(1)
         weigh(nc.vector, 1, 2)
         weigh(nc.vector, 1, 3)
-        unit(0, none, 2, 4)
-        ctl_transposes(1)
-        weigh_scalar(1, 0)
-        ctl_out(1)
-        weigh_scalar(1, 1)
-        ctl_quantize(1)
-        for t in (2, 3):
-            coef_passes(1, t)
-            coef_out(1, t)
+        weigh(nc.vector, 3, 3)
+        weigh_scalar(3, 0)
+        coef_passes(1, 3)
+        coef_out(1, 3)
         y_interleave(0)
         unit(1, none, 0, 2)
         coef_interleave(1)
@@ -342,7 +346,7 @@ def tile_frisch_waugh_partialling_k5_kernel(
         weigh_scalar(4, 1)
         weigh_scalar(4, 2)
         store_y(0)
-        load_treatments(0, 2, 3)
+        load_treatments(3)
         store_y(1)
         load_controls(3)
         unit(2, none, 0, 3)
@@ -351,15 +355,14 @@ def tile_frisch_waugh_partialling_k5_kernel(
         y_quantize(0)
         coef_out(2, 1)
         coef_out(2, 2)
-        y_interleave(2)
         store_y(2)
         store_codes(0)
         unit(3, [[], [], [], [(2, 3, g) for g in range(GROUPS)]])
         y_quantize(1)
         coef_out(2, 3)
+        y_interleave(2)
         store_y(3)
         store_codes(1)
-        load_treatments(3, 0, 3)
         y_interleave(3)
         unit(4, none, 0, 3)
         ctl_transposes(3)
@@ -371,7 +374,7 @@ def tile_frisch_waugh_partialling_k5_kernel(
         store_codes(2)
         store_y(4)
         y_interleave(4)
-        weigh_scalar(6, 2)
+        weigh_scalar(7, 2)
         last = len(UNITS) - 1
         for i in range(5, last):
             if i == 5:
@@ -383,8 +386,6 @@ def tile_frisch_waugh_partialling_k5_kernel(
             y_quantize(i - 2)
             store_y(i)
             store_codes(i - 2)
-            if i < last - 2:
-                weigh_scalar(i + 2, 2)
             y_interleave(i)
         unit(last, none)
         store_y(last, 0, 2)

@@ -17,27 +17,34 @@ ALU = mybir.AluOpType
 COPY = mybir.ActivationFunctionType.Copy
 
 P = 128
-PACK = 4
-GROUP = P * PACK
+SLOTS = 4
+GROUP = P * SLOTS
 GROUPS = N_OBS // GROUP
 CHUNK = 512
 CHUNKS = N_TRT // CHUNK
-UNITS = [(0, 0), (1, 0), (0, 1), (1, 1), (2, 0), (2, 1), (0, 2), (1, 2), (2, 2), (3, 0), (3, 1), (3, 2)]
-Y_SLOTS = 8
-GP = {
-    2: [(4, 3), (4, 0), (5, 0)],
-    3: [(5, 3), (5, 1), (5, 2)],
-    4: [(7, 3), (7, 0)],
-    5: [(8, 3), (7, 1)],
-    6: [(9, 3), (8, 0), (8, 1)],
-    7: [(10, 3), (8, 2), (9, 0)],
-    8: [(11, 3), (9, 1), (9, 2)],
-    9: [(10, 0), (10, 1), (10, 2)],
-    10: [(11, 0), (11, 1), (11, 2)],
+FP4_WORD = 2
+QUADRANT = 32
+SCALE_ROWS = 4
+PSUM_BANKS = 8
+
+SLICES = [(g, c, t) for c in range(CHUNKS) for g in (0, 1) for t in range(SLOTS)] + [
+    (g, c, t) for g in (2, 3) for t in range(SLOTS) for c in range(CHUNKS)
+]
+STRETCH = 4
+
+GPSIMD_WEIGHS = {
+    2: [(1, 2, 3, 1), (2, 0, 0, 2)],
+    3: [(2, 0, 1, 1), (2, 2, 0, 1)],
+    4: [(2, 1, 2, 1), (1, 2, 0, 1), (1, 2, 1, 1)],
+    5: [(2, 2, 3, 1), (2, 1, 1, 2)],
+    6: [(3, 0, 1, 1), (2, 0, 3, 2)],
+    7: [(3, 1, 2, 1), (3, 1, 1, 2)],
+    8: [(3, 0, 2, 1), (3, 0, 3, 2)],
+    9: [(3, 2, 2, 1), (3, 2, 3, 1)],
 }
-CODES = {0: 0, 1: 0, 2: 1, 3: 1, 5: 0, 6: 2, 7: 2, 8: 2, 10: 0, 11: 2}
-WARM = 3
-SPLIT = 3
+FIRST_SPARES = [(1, 0, 3), (0, 1, 3), (1, 1, 3), (0, 2, 3)]
+Y_RING = 4
+HALF = CHUNK // 2
 
 
 def tile_frisch_waugh_partialling_k5_kernel(
@@ -47,156 +54,162 @@ def tile_frisch_waugh_partialling_k5_kernel(
     with ExitStack() as ctx:
         keep = ctx.enter_context(tc.tile_pool(name="keep", bufs=1))
         turn = ctx.enter_context(tc.tile_pool(name="turn", bufs=2))
-        psum = ctx.enter_context(tc.psum_pool(name="psum", bufs=8))
+        psum = ctx.enter_context(tc.psum_pool(name="psum", bufs=PSUM_BANKS))
         ctx.enter_context(tc.manual_schedule())
 
         def kept(name, shape, dtype):
-            return keep.tile(shape, dtype, name=name, align_bytes=64)
+            return keep.tile(shape, dtype, name=name, tag=name, align_bytes=64)
 
         def bank(shape):
             return psum.tile(shape, F32, name="bank")
 
-        def cols(c):
-            return slice(c * CHUNK, (c + 1) * CHUNK)
+        def cols(c, n=1):
+            return slice(c * CHUNK, (c + n) * CHUNK)
 
         def rows(g):
             return slice(g * GROUP, (g + 1) * GROUP)
 
-        u_raw = kept("u_raw", [P, GROUPS, 2 * N_CTL], U8)
-        us_raw = kept("us_raw", [P, GROUPS, N_CTL], U8)
-        u_st = kept("u_st", [P, PACK, GROUPS, 2 * P], U8)
-        us_st = kept("us_st", [P, PACK, GROUPS, P], U8)
-        z_first = kept("z_first", [P, GROUPS, 2 * CHUNK], U8)
-        zs_first = kept("zs_first", [P, GROUPS, CHUNK], U8)
-        z_rest = kept("z_rest", [P, GROUPS, 2 * (N_TRT - CHUNK)], U8)
-        zs_rest = kept("zs_rest", [P, GROUPS, N_TRT - CHUNK], U8)
+        u_raw = kept("u_raw", [P, GROUPS, FP4_WORD * N_CTL], U8)
+        u_scale_raw = kept("u_scale_raw", [P, GROUPS, N_CTL], U8)
+        u_slots = kept("u_slots", [P, SLOTS, GROUPS, FP4_WORD * P], U8)
+        u_scale_slots = kept("u_scale_slots", [P, SLOTS, GROUPS, P], U8)
+        z_first = kept("z_first", [P, GROUPS, FP4_WORD * CHUNK], U8)
+        z_scale_first = kept("z_scale_first", [P, GROUPS, CHUNK], U8)
+        z_rest = kept("z_rest", [P, GROUPS, FP4_WORD * (N_TRT - CHUNK)], U8)
+        z_scale_rest = kept("z_scale_rest", [P, GROUPS, N_TRT - CHUNK], U8)
         vectors = kept("vectors", [P, GROUP], BF16)
-        norms32 = kept("norms32", [P, PACK], F32)
-        w32 = kept("w32", [P, GROUPS, PACK], F32)
-        negw32 = kept("negw32", [P, GROUPS, PACK], F32)
+        norms32 = kept("norms32", [P, SLOTS], F32)
+        weight32 = kept("weight32", [P, GROUPS, SLOTS], F32)
+        minus_weight32 = kept("minus_weight32", [P, GROUPS, SLOTS], F32)
         ident = kept("ident", [P, P], F32)
-        coef16 = kept("coef16", [P, PACK, CHUNK], BF16)
+        coef16 = kept("coef16", [P, SLOTS, CHUNK], BF16)
         coef_codes = [kept("coef_codes%d" % c, [P, CHUNK], U32) for c in range(CHUNKS)]
         coef_scales = [kept("coef_scales%d" % c, [P, CHUNK], U8) for c in range(CHUNKS)]
         ctl_codes = [kept("ctl_codes%d" % g, [P, GROUP], U32) for g in range(GROUPS)]
         ctl_scales = [kept("ctl_scales%d" % g, [P, GROUP], U8) for g in range(GROUPS)]
-        y_slots = [kept("y32_%d" % i, [P, PACK, CHUNK], F32) for i in range(Y_SLOTS)]
-        y32 = [y_slots[i % Y_SLOTS] for i in range(len(UNITS))]
-        side = {(i, 3): kept("side%d" % i, [P, CHUNK], F32)[:] for i in (1, 2, 3, 6)}
+
+        y_reused = kept("y_reused", [P, SLOTS * N_TRT], F32)
+        y_chunk = {key: kept("y_%d%d" % key, [P, SLOTS, CHUNK], F32)[:] for key in ((1, 1), (0, 2), (1, 2))}
+        y_pair = y_reused[:, : 2 * SLOTS * CHUNK].rearrange("p (t m) -> p t m", t=SLOTS)
+        y_chunk[0, 0] = y_pair[:, :, cols(0)]
+        y_chunk[0, 1] = y_pair[:, :, cols(1)]
+        y_chunk[1, 0] = y_reused[:, 2 * SLOTS * CHUNK :].rearrange("p (t m) -> p t m", t=SLOTS)
+        y_rows = {3: y_reused[:].rearrange("p (t m) -> p t m", t=SLOTS)}
+        spare = {key: kept("spare%d%d%d" % key, [P, CHUNK], F32)[:] for key in FIRST_SPARES}
         y_codes = [kept("y_codes%d" % g, [P, N_TRT], U32) for g in range(GROUPS)]
         y_scales = kept("y_scales", [P, N_TRT], U8)
-        trt = [kept("trt%d" % g, [P, PACK, N_TRT], BF16) for g in range(GROUPS)]
+        trt = [kept("trt%d" % g, [P, SLOTS, N_TRT], BF16) for g in range(GROUPS)]
         ctl_raw = {}
         coef_bank = {}
-        ctl_bank = {}
-        fit_bank = {}
-        ctl_pair = [kept("ctl_grouped%d" % n, [P, GROUP * PACK], BF16) for n in range(2)]
-        ctl_grouped = [ctl_pair[g % 2] for g in range(GROUPS)]
-        coef_one = kept("coef_grouped", [P, CHUNK * PACK], BF16)
-        coef_grouped = [coef_one] * CHUNKS
-        y_ring = [kept("y_grouped%d" % n, [P, CHUNK * PACK], BF16) for n in range(3)]
-        y_grouped = [y_ring[i % 3] for i in range(len(UNITS))]
+        ctl_words = [kept("ctl_words%d" % n, [P, GROUP * SLOTS], BF16) for n in range(2)]
+        coef_words = kept("coef_words", [P, CHUNK * SLOTS], BF16)
+        y_ring = [kept("y_words%d" % n, [P, CHUNK * SLOTS], BF16) for n in range(Y_RING)]
+        finished = [(g, c) for c in range(CHUNKS) for g in (0, 1)] + [(g, c) for g in (2, 3) for c in range(CHUNKS)]
+        y_words = {key: y_ring[n % Y_RING] for n, key in enumerate(finished)}
 
-        def load_scale_rows(queue, plane, src, c0, c1, rs=range(4)):
-            view = src.rearrange("g (q r) n -> r q g n", r=4)
-            for r in rs:
-                queue.dma_start(out=plane[r:P:32].bitcast(I32), in_=view[r][:, :, c0:c1].bitcast(I32))
 
-        def load_words(dst, src, b0, b1, g0=0, g1=GROUPS):
-            view = src.rearrange("g p b -> p g b")[:, g0:g1, b0:b1]
+        def load_scale_rows(plane, src, first, last):
+            view = src.rearrange("g (q r) n -> r q g n", r=SCALE_ROWS)
+            for r in range(SCALE_ROWS):
+                nc.sync.dma_start(out=plane[r:P:QUADRANT].bitcast(I32), in_=view[r][:, :, first:last].bitcast(I32))
+
+        def load_words(dst, src, first, last, g0=0, g1=GROUPS):
+            view = src.rearrange("g p b -> p g b")[:, g0:g1, FP4_WORD * first : FP4_WORD * last]
             nc.sync.dma_start(out=dst[:, g0:g1, :].bitcast(I32), in_=view.bitcast(I32))
 
         def load_controls(g):
-            ctl_raw[g] = turn.tile([P, PACK, N_CTL], BF16, name="ctl_raw", align_bytes=64)
-            nc.sync.dma_start(out=ctl_raw[g][:], in_=controls[rows(g), :].rearrange("(m t) k -> m t k", t=PACK))
+            ctl_raw[g] = turn.tile([P, SLOTS, N_CTL], BF16, name="ctl_raw", align_bytes=64)
+            nc.sync.dma_start(out=ctl_raw[g][:], in_=controls[rows(g), :].rearrange("(m t) k -> m t k", t=SLOTS))
 
-        def load_treatments(g, t0=0, t1=PACK):
-            src = treatments[rows(g), :].rearrange("(p t) m -> p t m", t=PACK)
+        def load_treatments(g, t0=0, t1=SLOTS):
+            src = treatments[rows(g), :].rearrange("(p t) m -> p t m", t=SLOTS)
             nc.sync.dma_start(out=trt[g][:, t0:t1, :], in_=src[:, t0:t1, :])
 
-        def order_u(t):
+
+        def gather_u_slot(t):
             nc.vector.tensor_copy(
-                out=u_st[:, t].rearrange("p g (m b) -> p g m b", b=2),
-                in_=u_raw[:].rearrange("p g (m t b) -> p t g m b", t=PACK, b=2)[:, t],
+                out=u_slots[:, t].rearrange("p g (m b) -> p g m b", b=FP4_WORD),
+                in_=u_raw[:].rearrange("p g (m t b) -> p t g m b", t=SLOTS, b=FP4_WORD)[:, t],
             )
-            nc.vector.tensor_copy(out=us_st[:, t], in_=us_raw[:].rearrange("p g (m t) -> p t g m", t=PACK)[:, t])
-
-        def coef_pass(c, t, g):
-            if g == 0:
-                coef_bank[c, t] = bank([P, CHUNK])
-            if c == 0:
-                zw, zs = z_first[:, g, :], zs_first[:, g, :]
-            else:
-                zw = z_rest[:, g, 2 * (c - 1) * CHUNK : 2 * c * CHUNK]
-                zs = zs_rest[:, g, (c - 1) * CHUNK : c * CHUNK]
-            nc.tensor.matmul_mx(
-                out=coef_bank[c, t][:],
-                lhsT=u_st[:, t, g, :].bitcast(FP4X4),
-                lhsT_scale=us_st[:, t, g, :],
-                rhs=zw.bitcast(FP4X4),
-                rhs_scale=zs,
-                start=(g == 0),
-                stop=(g == GROUPS - 1),
+            nc.vector.tensor_copy(
+                out=u_scale_slots[:, t], in_=u_scale_raw[:].rearrange("p g (m t) -> p t g m", t=SLOTS)[:, t]
             )
 
-        def coef_passes(c, t):
-            for g in range(GROUPS):
-                coef_pass(c, t, g)
+        def coef_passes(c, t, g0=0, g1=GROUPS):
+            for g in range(g0, g1):
+                if g == 0:
+                    coef_bank[c, t] = bank([P, CHUNK])
+                if c == 0:
+                    z_tile, z_scale = z_first[:, g, :], z_scale_first[:, g, :]
+                else:
+                    z_tile = z_rest[:, g, FP4_WORD * (c - 1) * CHUNK : FP4_WORD * c * CHUNK]
+                    z_scale = z_scale_rest[:, g, cols(c - 1)]
+                nc.tensor.matmul_mx(
+                    out=coef_bank[c, t][:],
+                    lhsT=u_slots[:, t, g, :].bitcast(FP4X4),
+                    lhsT_scale=u_scale_slots[:, t, g, :],
+                    rhs=z_tile.bitcast(FP4X4),
+                    rhs_scale=z_scale,
+                    start=(g == 0),
+                    stop=(g == GROUPS - 1),
+                )
 
         def coef_out(c, t):
             nc.scalar.activation(out=coef16[:, t, :], in_=coef_bank[c, t][:], func=COPY, scale=norms32[:, t : t + 1])
 
-        def coef_interleave(c):
+        def coef_interleave():
             nc.vector.tensor_copy(
-                out=coef_grouped[c][:].rearrange("p (n i t) -> p n t i", i=4, t=PACK),
+                out=coef_words[:].rearrange("p (n i t) -> p n t i", i=4, t=SLOTS),
                 in_=coef16[:].rearrange("p t (n i) -> p n t i", i=4),
             )
 
         def coef_quantize(c):
-            nc.vector.quantize_mx(out=coef_codes[c][:].bitcast(FP8X4), scales=coef_scales[c][:], in_=coef_grouped[c][:])
+            nc.vector.quantize_mx(out=coef_codes[c][:].bitcast(FP8X4), scales=coef_scales[c][:], in_=coef_words[:])
 
-        def ctl_transposes(g, hs=(0, 1)):
-            words = ctl_raw[g][:].bitcast(F32)
-            for h in hs:
-                ctl_bank[g, h] = bank([P, 2, 2, P])
+
+        def ctl_transpose(g):
+            pairs = ctl_raw[g][:].bitcast(F32)
+            banks = []
+            for h in range(2):
+                banks.append(bank([P, 2, 2, P]))
                 for a in range(2):
                     for u in range(2):
-                        nc.tensor.transpose(ctl_bank[g, h][:, a, u, :], words[:, 2 * h + a, u : 2 * P : 2], ident[:])
-
-        def ctl_out(g, hs=(0, 1)):
-            dst = ctl_grouped[g][:].bitcast(F32).rearrange("p (h a m u) -> p h a m u", h=2, a=2, u=2)
-            for h in hs:
-                nc.scalar.copy(out=dst[:, h], in_=ctl_bank[g, h][:].rearrange("p a u m -> p a m u"))
+                        nc.tensor.transpose(banks[h][:, a, u, :], pairs[:, 2 * h + a, u : 2 * P : 2], ident[:])
+            dst = ctl_words[g % 2][:].bitcast(F32).rearrange("p (h a m u) -> p h a m u", h=2, a=2, u=2)
+            for h in range(2):
+                nc.scalar.copy(out=dst[:, h], in_=banks[h][:].rearrange("p a u m -> p a m u"))
 
         def ctl_quantize(g):
-            nc.vector.quantize_mx(out=ctl_codes[g][:].bitcast(FP8X4), scales=ctl_scales[g][:], in_=ctl_grouped[g][:])
+            nc.vector.quantize_mx(out=ctl_codes[g][:].bitcast(FP8X4), scales=ctl_scales[g][:], in_=ctl_words[g % 2][:])
 
-        def weighed(i, t):
-            return side.get((i, t), y32[i][:, t, :])
 
-        def weigh(engine, i, t):
-            g, c = UNITS[i]
+        def y_slice(g, c, t, n=1):
+            if g in y_rows:
+                return y_rows[g][:, t, cols(c, n)]
+            return y_chunk[g, c][:, t, :]
+
+        def weighed(g, c, t, n=1):
+            return spare.get((g, c, t), y_slice(g, c, t, n))
+
+        def weigh(engine, g, c, t, n=1):
             engine.tensor_scalar(
-                out=weighed(i, t), in0=trt[g][:, t, cols(c)], scalar1=w32[:, g, t : t + 1], scalar2=0.0,
-                op0=ALU.mult, op1=ALU.add,
+                out=weighed(g, c, t, n),
+                in0=trt[g][:, t, cols(c, n)],
+                scalar1=weight32[:, g, t : t + 1],
+                scalar2=0.0,
+                op0=ALU.mult,
+                op1=ALU.add,
             )
 
-        def weigh_scalar(i, t):
-            g, c = UNITS[i]
-            nc.scalar.activation(out=weighed(i, t), in_=trt[g][:, t, cols(c)], func=COPY, scale=w32[:, g, t : t + 1])
+        def weigh_on_scalar(g, c, t, n=1):
+            nc.scalar.activation(
+                out=weighed(g, c, t, n), in_=trt[g][:, t, cols(c, n)], func=COPY, scale=weight32[:, g, t : t + 1]
+            )
 
-        def weigh_beside(j):
-            steps = GP.get(j, [])
-            if steps:
-                side[steps[0]] = side[j - 1, 3]
-            for i, t in steps:
-                weigh(nc.gpsimd, i, t)
-
-        def fit(i, t):
-            g, c = UNITS[i]
-            fit_bank[i, t] = bank([P, CHUNK])
+        def residual(g, c, t):
+            fitted = bank([P, CHUNK])
             nc.tensor.matmul_mx(
-                out=fit_bank[i, t][:],
+                out=fitted[:],
                 lhsT=ctl_codes[g][:, t * P : (t + 1) * P].bitcast(FP8X4),
                 lhsT_scale=ctl_scales[g][:, t * P : (t + 1) * P],
                 rhs=coef_codes[c][:].bitcast(FP8X4),
@@ -204,201 +217,190 @@ def tile_frisch_waugh_partialling_k5_kernel(
                 start=True,
                 stop=True,
             )
-
-        def residual(i, t):
-            g = UNITS[i][0]
             nc.vector.scalar_tensor_tensor(
-                out=y32[i][:, t, :], in0=fit_bank[i, t][:], scalar=negw32[:, g, t : t + 1], in1=weighed(i, t),
-                op0=ALU.mult, op1=ALU.add,
+                out=y_slice(g, c, t),
+                in0=fitted[:],
+                scalar=minus_weight32[:, g, t : t + 1],
+                in1=weighed(g, c, t),
+                op0=ALU.mult,
+                op1=ALU.add,
             )
+            if g in y_rows and c == CHUNKS - 1:
+                dst = out_0[rows(g), :].rearrange("(p t) m -> p t m", t=SLOTS)
+                nc.sync.dma_start(out=dst[:, t : t + 1, :], in_=y_rows[g][:, t : t + 1, :])
 
-        def unit(i, beside, t0=0, t1=PACK):
-            if t0 == 0:
-                weigh_beside(i)
-            for t in range(t0, t1):
-                fit(i, t)
-                residual(i, t)
-                for step in beside[t - t0]:
-                    coef_pass(*step)
+        def stretch(j, first=0, last=STRETCH):
+            if first == 0 and j in GPSIMD_WEIGHS:
+                spare[GPSIMD_WEIGHS[j][0][:3]] = spare[SLICES[STRETCH * j - 1]]
+                for step in GPSIMD_WEIGHS[j]:
+                    weigh(nc.gpsimd, *step)
+            for n in range(first, last):
+                residual(*SLICES[STRETCH * j + n])
 
-        def y_interleave(i, h0=0, h1=8, copy=nc.scalar.copy):
-            half = CHUNK // 8
-            src = y32[i][:, :, h0 * half : h1 * half]
-            dst = y_grouped[i][:, h0 * half * PACK : h1 * half * PACK]
+        def y_interleave(g, c, first=0, last=CHUNK, copy=nc.scalar.copy):
+            whole = y_rows[g][:, :, cols(c)] if g in y_rows else y_chunk[g, c]
             copy(
-                out=dst.rearrange("p (n i t) -> p n t i", i=2, t=PACK),
-                in_=src.rearrange("p t (n i) -> p n t i", i=2),
+                out=y_words[g, c][:, first * SLOTS : last * SLOTS].rearrange("p (n i t) -> p n t i", i=2, t=SLOTS),
+                in_=whole[:, :, first:last].rearrange("p t (n i) -> p n t i", i=2),
             )
 
-        def y_quantize(i):
-            g, c = UNITS[i]
+        def y_quantize(g, c):
             nc.vector.quantize_mx(
-                out=y_codes[g][:, cols(c)].bitcast(FP8X4), scales=y_scales[4 * g : P, cols(c)], in_=y_grouped[i][:]
+                out=y_codes[g][:, cols(c)].bitcast(FP8X4),
+                scales=y_scales[SCALE_ROWS * g : P, cols(c)],
+                in_=y_words[g, c][:],
             )
 
-        def store_y(i, t0=0, t1=PACK):
-            g, c = UNITS[i]
-            dst = out_0[rows(g), cols(c)].rearrange("(p t) m -> p t m", t=PACK)
-            nc.sync.dma_start(out=dst[:, t0:t1, :], in_=y32[i][:, t0:t1, :])
+        def store_y(g, c, src, n=1):
+            nc.sync.dma_start(out=out_0[rows(g), cols(c, n)].rearrange("(p t) m -> p t m", t=SLOTS), in_=src)
 
-        def store_codes(i):
-            if i not in CODES:
-                return
-            g, c = UNITS[i]
+        def store_codes(g, c, n=1):
             dst = out_1[g].rearrange("p m t -> p (m t)").bitcast(I32)
-            span = slice(CODES[i] * CHUNK, (c + 1) * CHUNK)
-            nc.sync.dma_start(out=dst[:, span], in_=y_codes[g][:, span].bitcast(I32))
+            nc.sync.dma_start(out=dst[:, cols(c, n)], in_=y_codes[g][:, cols(c, n)].bitcast(I32))
 
         nc.vector.memset(vectors[:].bitcast(I32), 0)
-        nc.vector.memset(zs_first[:].bitcast(I32), 0)
-        nc.vector.memset(us_raw[:].bitcast(I32), 0)
-        nc.vector.memset(zs_rest[:].bitcast(I32), 0)
+        nc.vector.memset(z_scale_first[:].bitcast(I32), 0)
+        nc.vector.memset(u_scale_raw[:].bitcast(I32), 0)
+        nc.vector.memset(z_scale_rest[:].bitcast(I32), 0)
         make_identity(nc, ident[:])
-        load_words(u_raw, u_words, 0, 2 * N_CTL)
+
+        load_words(u_raw, u_words, 0, N_CTL)
         nc.sync.dma_start(out=vectors[0:GROUPS, :], in_=row_weight.rearrange("(g k) -> g k", g=GROUPS))
         nc.sync.dma_start(out=vectors[GROUPS : GROUPS + 1, :], in_=norms.rearrange("(o k) -> o k", o=1))
-        load_scale_rows(nc.sync, us_raw, u_scales, 0, N_CTL)
-        load_words(z_first, z_words, 0, 2 * CHUNK)
-        load_scale_rows(nc.sync, zs_first, z_scales, 0, CHUNK)
+        load_scale_rows(u_scale_raw, u_scales, 0, N_CTL)
+        load_words(z_first, z_words, 0, CHUNK)
+        load_scale_rows(z_scale_first, z_scales, 0, CHUNK)
         load_treatments(0, 0, 2)
         load_controls(0)
-        load_scale_rows(nc.sync, zs_rest, z_scales, CHUNK, N_TRT)
-        load_words(z_rest, z_words, 2 * CHUNK, 2 * N_TRT, 0, 2)
-        load_words(z_rest, z_words, 2 * CHUNK, 2 * N_TRT, 2, 4)
         load_treatments(0, 2, 4)
+        load_scale_rows(z_scale_rest, z_scales, CHUNK, N_TRT)
+        load_words(z_rest, z_words, CHUNK, N_TRT, 0, 2)
+        load_words(z_rest, z_words, CHUNK, N_TRT, 2, 4)
         load_controls(1)
         load_treatments(1, 0, 2)
         load_treatments(1, 2, 4)
 
-        none = [[]] * PACK
-        vec_bank = bank([P, 2, P])
+        vector_bank = bank([P, 2, P])
         for u in range(2):
-            nc.tensor.transpose(vec_bank[:, u, :], vectors[:].bitcast(F32)[:, u : 2 * P : 2], ident[:])
-        turned = vec_bank[:].bitcast(BF16).rearrange("p u (j e) -> p j u e", e=2)
+            nc.tensor.transpose(vector_bank[:, u, :], vectors[:].bitcast(F32)[:, u : 2 * P : 2], ident[:])
+        turned = vector_bank[:].bitcast(BF16).rearrange("p u (j e) -> p j u e", e=2)
         nc.scalar.activation(out=norms32[:].rearrange("p (u e) -> p u e", e=2), in_=turned[:, GROUPS], func=COPY)
-        nc.scalar.activation(out=w32[:].rearrange("p g (u e) -> p g u e", e=2), in_=turned[:, :GROUPS], func=COPY)
+        nc.scalar.activation(out=weight32[:].rearrange("p g (u e) -> p g u e", e=2), in_=turned[:, :GROUPS], func=COPY)
         nc.scalar.activation(
-            out=negw32[:].rearrange("p g (u e) -> p g u e", e=2), in_=turned[:, :GROUPS], func=COPY, scale=-1.0
+            out=minus_weight32[:].rearrange("p g (u e) -> p g u e", e=2), in_=turned[:, :GROUPS], func=COPY, scale=-1.0
         )
-        warm_bank = bank([P, CHUNK])
-        for n in range(WARM):
-            nc.tensor.matmul_mx(
-                out=warm_bank[:],
-                lhsT=u_raw[:, 0, : 2 * P].bitcast(FP4X4),
-                lhsT_scale=us_raw[:, 0, :P],
-                rhs=u_raw[:, 0, :].bitcast(FP4X4),
-                rhs_scale=us_raw[:, 0, :],
-                start=True,
-                stop=True,
-            )
-        for t in range(PACK):
-            order_u(t)
-        for t in range(2):
-            for i in (0, 2, 6):
-                weigh(nc.vector, i, t)
-        for t in range(PACK):
+
+        for t in range(SLOTS):
+            gather_u_slot(t)
+        for t in range(SLOTS):
+            for c in range(CHUNKS):
+                weigh(nc.vector, 0, c, t)
+        for t in range(SLOTS):
             coef_passes(0, t)
             coef_out(0, t)
-        ctl_transposes(0)
-        ctl_out(0)
+        ctl_transpose(0)
         load_controls(2)
         load_treatments(2)
-        coef_interleave(0)
+        coef_interleave()
         ctl_quantize(0)
         coef_quantize(0)
-        weigh(nc.vector, 0, 2)
-        weigh(nc.vector, 0, 3)
+
         for t in range(2):
-            coef_pass(1, t, 0)
-            coef_pass(1, t, 1)
+            coef_passes(1, t, 0, 2)
         for t in range(2):
-            coef_pass(1, t, 2)
-            coef_pass(1, t, 3)
+            coef_passes(1, t, 2, 4)
             coef_out(1, t)
-        for t in range(PACK):
-            unit(0, [[(1, 2, t)]], t, t + 1)
-            weigh(nc.vector, (2, 6)[t % 2], 2 + t // 2)
-        coef_out(1, 2)
-        ctl_transposes(1)
-        ctl_out(1)
-        weigh(nc.vector, 1, 0)
-        weigh(nc.vector, 1, 1)
+        stretch(0)
+        ctl_transpose(1)
+        weigh(nc.vector, 1, 0, 0)
+        weigh(nc.vector, 1, 0, 1)
         ctl_quantize(1)
-        weigh(nc.vector, 1, 2)
-        weigh(nc.vector, 1, 3)
-        weigh(nc.vector, 3, 3)
-        weigh_scalar(3, 0)
-        coef_passes(1, 3)
-        coef_out(1, 3)
-        y_interleave(0)
-        unit(1, none, 0, 2)
-        coef_interleave(1)
-        unit(1, none, 2, 3)
+        weigh(nc.vector, 1, 0, 2)
+        weigh(nc.vector, 1, 0, 3)
+        weigh(nc.vector, 1, 1, 3)
+        for t in range(2):
+            weigh_on_scalar(1, 1, t)
+            coef_passes(1, 2 + t)
+            coef_out(1, 2 + t)
+        y_interleave(0, 0)
+        stretch(1, 0, 1)
+        coef_interleave()
+        stretch(1, 1, 2)
         coef_quantize(1)
-        unit(1, none, 3, 4)
-        coef_passes(2, 0)
-        coef_out(2, 0)
-        weigh_scalar(3, 1)
-        weigh_scalar(3, 2)
-        ctl_transposes(2)
-        ctl_out(2)
-        y_interleave(1)
-        weigh_scalar(4, 1)
-        weigh_scalar(4, 2)
-        store_y(0)
+        stretch(1, 2, 4)
+
+        for t in range(2):
+            coef_passes(2, t)
+            coef_out(2, t)
+        weigh_on_scalar(1, 1, 2)
         load_treatments(3)
-        store_y(1)
         load_controls(3)
-        unit(2, none, 0, 3)
-        ctl_quantize(2)
-        unit(2, [[(2, t, g) for t in (1, 2) for g in range(GROUPS)]], 3, 4)
-        y_quantize(0)
-        coef_out(2, 1)
+        store_y(1, 0, y_chunk[1, 0])
+        y_rows[2] = keep.tile([P, SLOTS, N_TRT], F32, name="y_rows2", tag="trt0", align_bytes=64)[:]
+        y_interleave(1, 0, 0, HALF)
+        stretch(2)
+        coef_passes(2, 2)
+        coef_passes(2, 3)
+        y_quantize(0, 0)
         coef_out(2, 2)
-        store_y(2)
-        store_codes(0)
-        unit(3, [[], [], [], [(2, 3, g) for g in range(GROUPS)]])
-        y_quantize(1)
         coef_out(2, 3)
-        y_interleave(2)
-        store_y(3)
-        store_codes(1)
-        y_interleave(3)
-        unit(4, none, 0, 3)
-        ctl_transposes(3)
-        ctl_out(3)
-        coef_interleave(2)
-        y_quantize(2)
-        unit(4, none, 3, 4)
+        y_interleave(1, 0, HALF, CHUNK)
+        store_y(0, 0, y_pair, 2)
+        store_codes(0, 0)
+        stretch(3, 0, 3)
+        ctl_transpose(2)
+        coef_interleave()
+        ctl_quantize(2)
         coef_quantize(2)
-        store_codes(2)
-        store_y(4)
-        y_interleave(4)
-        weigh_scalar(7, 2)
-        last = len(UNITS) - 1
-        for i in range(5, last):
-            if i == 5:
-                unit(i, none, 0, 3)
-                ctl_quantize(3)
-                unit(i, none, 3, 4)
-            else:
-                unit(i, none)
-            y_quantize(i - 2)
-            store_y(i)
-            store_codes(i - 2)
-            y_interleave(i)
-        unit(last, none)
-        store_y(last, 0, 2)
-        store_y(last, 2, 4)
-        y_quantize(last - 2)
-        store_codes(last - 2)
-        y_interleave(last, 0, SPLIT)
-        y_interleave(last, SPLIT, 8, nc.vector.tensor_copy)
-        y_quantize(last - 1)
-        store_codes(last - 1)
-        y_quantize(last)
-        store_codes(last)
-        for q in range(4):
+        stretch(3, 3, 4)
+        y_quantize(1, 0)
+        store_y(1, 1, y_chunk[1, 1])
+        store_codes(1, 0)
+        y_interleave(0, 1)
+        weigh_on_scalar(1, 2, 2)
+        y_interleave(1, 1)
+
+        stretch(4)
+        y_quantize(0, 1)
+        store_codes(0, 1)
+        store_y(0, 2, y_chunk[0, 2])
+        weigh_on_scalar(2, 0, 2)
+        y_interleave(0, 2)
+        stretch(5)
+        ctl_transpose(3)
+        y_quantize(1, 1)
+        store_y(1, 2, y_chunk[1, 2])
+        weigh_on_scalar(2, 2, 2)
+        y_interleave(1, 2)
+        weigh_on_scalar(3, 0, 0, CHUNKS)
+
+        stretch(6)
+        y_quantize(0, 2)
+        store_codes(0, 2)
+        stretch(7)
+        ctl_quantize(3)
+        stretch(8)
+        y_quantize(1, 2)
+        store_codes(1, 1, 2)
+        for c in range(CHUNKS):
+            y_interleave(2, c)
+
+        for c in range(CHUNKS):
+            stretch(9 + c)
+            y_quantize(2, c)
+        store_codes(2, 0, CHUNKS)
+
+        y_interleave(3, 0)
+        y_interleave(3, 1, 0, HALF)
+        y_interleave(3, 2, 0, CHUNK, nc.vector.tensor_copy)
+        y_interleave(3, 1, HALF, CHUNK, nc.vector.tensor_copy)
+        y_quantize(3, 0)
+        store_codes(3, 0)
+        y_quantize(3, 2)
+        y_quantize(3, 1)
+        store_codes(3, 1, 2)
+        for q in range(P // QUADRANT):
             nc.sync.dma_start(
-                out=out_2[:, 4 * q : 4 * q + 4, :].bitcast(I32), in_=y_scales[32 * q : 32 * q + 16, :].bitcast(I32)
+                out=out_2[:, SCALE_ROWS * q : SCALE_ROWS * (q + 1), :].bitcast(I32),
+                in_=y_scales[QUADRANT * q : QUADRANT * q + SCALE_ROWS * GROUPS, :].bitcast(I32),
             )

from contextlib import ExitStack

import concourse.mybir as mybir
from concourse.masks import make_identity

N_OBS, N_CTL, N_TRT = 2048, 512, 1536
FLOPS = 2 * N_OBS * N_CTL * N_TRT * 2

F32 = mybir.dt.float32
BF16 = mybir.dt.bfloat16
I32 = mybir.dt.int32
U32 = mybir.dt.uint32
U8 = mybir.dt.uint8
FP8X4 = mybir.dt.float8_e4m3fn_x4
FP4X4 = mybir.dt.float4_e2m1fn_x4
ALU = mybir.AluOpType
COPY = mybir.ActivationFunctionType.Copy

P = 128
SLOTS = 4
GROUP = P * SLOTS
GROUPS = N_OBS // GROUP
CHUNK = 512
CHUNKS = N_TRT // CHUNK
FP4_WORD = 2
QUADRANT = 32
SCALE_ROWS = 4
PSUM_BANKS = 8

SLICES = [(g, c, t) for c in range(CHUNKS) for g in (0, 1) for t in range(SLOTS)] + [
    (g, c, t) for g in (2, 3) for t in range(SLOTS) for c in range(CHUNKS)
]
STRETCH = 4

GPSIMD_WEIGHS = {
    2: [(1, 2, 3, 1), (2, 0, 0, 2)],
    3: [(2, 0, 1, 1), (2, 2, 0, 1)],
    4: [(2, 1, 2, 1), (1, 2, 0, 1), (1, 2, 1, 1)],
    5: [(2, 2, 3, 1), (2, 1, 1, 2)],
    6: [(3, 0, 1, 1), (2, 0, 3, 2)],
    7: [(3, 1, 2, 1), (3, 1, 1, 2)],
    8: [(3, 0, 2, 1), (3, 0, 3, 2)],
    9: [(3, 2, 2, 1), (3, 2, 3, 1)],
}
FIRST_SPARES = [(1, 0, 3), (0, 1, 3), (1, 1, 3), (0, 2, 3)]
Y_RING = 4
HALF = CHUNK // 2


def tile_frisch_waugh_partialling_k5_kernel(
    tc, u_words, u_scales, z_words, z_scales, norms, controls, treatments, row_weight, out_0, out_1, out_2
):
    nc = tc.nc
    with ExitStack() as ctx:
        keep = ctx.enter_context(tc.tile_pool(name="keep", bufs=1))
        turn = ctx.enter_context(tc.tile_pool(name="turn", bufs=2))
        psum = ctx.enter_context(tc.psum_pool(name="psum", bufs=PSUM_BANKS))
        ctx.enter_context(tc.manual_schedule())

        def kept(name, shape, dtype):
            return keep.tile(shape, dtype, name=name, tag=name, align_bytes=64)

        def bank(shape):
            return psum.tile(shape, F32, name="bank")

        def cols(c, n=1):
            return slice(c * CHUNK, (c + n) * CHUNK)

        def rows(g):
            return slice(g * GROUP, (g + 1) * GROUP)

        u_raw = kept("u_raw", [P, GROUPS, FP4_WORD * N_CTL], U8)
        u_scale_raw = kept("u_scale_raw", [P, GROUPS, N_CTL], U8)
        u_slots = kept("u_slots", [P, SLOTS, GROUPS, FP4_WORD * P], U8)
        u_scale_slots = kept("u_scale_slots", [P, SLOTS, GROUPS, P], U8)
        z_first = kept("z_first", [P, GROUPS, FP4_WORD * CHUNK], U8)
        z_scale_first = kept("z_scale_first", [P, GROUPS, CHUNK], U8)
        z_rest = kept("z_rest", [P, GROUPS, FP4_WORD * (N_TRT - CHUNK)], U8)
        z_scale_rest = kept("z_scale_rest", [P, GROUPS, N_TRT - CHUNK], U8)
        vectors = kept("vectors", [P, GROUP], BF16)
        norms32 = kept("norms32", [P, SLOTS], F32)
        weight32 = kept("weight32", [P, GROUPS, SLOTS], F32)
        minus_weight32 = kept("minus_weight32", [P, GROUPS, SLOTS], F32)
        ident = kept("ident", [P, P], F32)
        coef16 = kept("coef16", [P, SLOTS, CHUNK], BF16)
        coef_codes = [kept("coef_codes%d" % c, [P, CHUNK], U32) for c in range(CHUNKS)]
        coef_scales = [kept("coef_scales%d" % c, [P, CHUNK], U8) for c in range(CHUNKS)]
        ctl_codes = [kept("ctl_codes%d" % g, [P, GROUP], U32) for g in range(GROUPS)]
        ctl_scales = [kept("ctl_scales%d" % g, [P, GROUP], U8) for g in range(GROUPS)]

        y_reused = kept("y_reused", [P, SLOTS * N_TRT], F32)
        y_chunk = {key: kept("y_%d%d" % key, [P, SLOTS, CHUNK], F32)[:] for key in ((1, 1), (0, 2), (1, 2))}
        y_pair = y_reused[:, : 2 * SLOTS * CHUNK].rearrange("p (t m) -> p t m", t=SLOTS)
        y_chunk[0, 0] = y_pair[:, :, cols(0)]
        y_chunk[0, 1] = y_pair[:, :, cols(1)]
        y_chunk[1, 0] = y_reused[:, 2 * SLOTS * CHUNK :].rearrange("p (t m) -> p t m", t=SLOTS)
        y_rows = {3: y_reused[:].rearrange("p (t m) -> p t m", t=SLOTS)}
        spare = {key: kept("spare%d%d%d" % key, [P, CHUNK], F32)[:] for key in FIRST_SPARES}
        y_codes = [kept("y_codes%d" % g, [P, N_TRT], U32) for g in range(GROUPS)]
        y_scales = kept("y_scales", [P, N_TRT], U8)
        trt = [kept("trt%d" % g, [P, SLOTS, N_TRT], BF16) for g in range(GROUPS)]
        ctl_raw = {}
        coef_bank = {}
        ctl_words = [kept("ctl_words%d" % n, [P, GROUP * SLOTS], BF16) for n in range(2)]
        coef_words = kept("coef_words", [P, CHUNK * SLOTS], BF16)
        y_ring = [kept("y_words%d" % n, [P, CHUNK * SLOTS], BF16) for n in range(Y_RING)]
        finished = [(g, c) for c in range(CHUNKS) for g in (0, 1)] + [(g, c) for g in (2, 3) for c in range(CHUNKS)]
        y_words = {key: y_ring[n % Y_RING] for n, key in enumerate(finished)}


        def load_scale_rows(plane, src, first, last):
            view = src.rearrange("g (q r) n -> r q g n", r=SCALE_ROWS)
            for r in range(SCALE_ROWS):
                nc.sync.dma_start(out=plane[r:P:QUADRANT].bitcast(I32), in_=view[r][:, :, first:last].bitcast(I32))

        def load_words(dst, src, first, last, g0=0, g1=GROUPS):
            view = src.rearrange("g p b -> p g b")[:, g0:g1, FP4_WORD * first : FP4_WORD * last]
            nc.sync.dma_start(out=dst[:, g0:g1, :].bitcast(I32), in_=view.bitcast(I32))

        def load_controls(g):
            ctl_raw[g] = turn.tile([P, SLOTS, N_CTL], BF16, name="ctl_raw", align_bytes=64)
            nc.sync.dma_start(out=ctl_raw[g][:], in_=controls[rows(g), :].rearrange("(m t) k -> m t k", t=SLOTS))

        def load_treatments(g, t0=0, t1=SLOTS):
            src = treatments[rows(g), :].rearrange("(p t) m -> p t m", t=SLOTS)
            nc.sync.dma_start(out=trt[g][:, t0:t1, :], in_=src[:, t0:t1, :])


        def gather_u_slot(t):
            nc.vector.tensor_copy(
                out=u_slots[:, t].rearrange("p g (m b) -> p g m b", b=FP4_WORD),
                in_=u_raw[:].rearrange("p g (m t b) -> p t g m b", t=SLOTS, b=FP4_WORD)[:, t],
            )
            nc.vector.tensor_copy(
                out=u_scale_slots[:, t], in_=u_scale_raw[:].rearrange("p g (m t) -> p t g m", t=SLOTS)[:, t]
            )

        def coef_passes(c, t, g0=0, g1=GROUPS):
            for g in range(g0, g1):
                if g == 0:
                    coef_bank[c, t] = bank([P, CHUNK])
                if c == 0:
                    z_tile, z_scale = z_first[:, g, :], z_scale_first[:, g, :]
                else:
                    z_tile = z_rest[:, g, FP4_WORD * (c - 1) * CHUNK : FP4_WORD * c * CHUNK]
                    z_scale = z_scale_rest[:, g, cols(c - 1)]
                nc.tensor.matmul_mx(
                    out=coef_bank[c, t][:],
                    lhsT=u_slots[:, t, g, :].bitcast(FP4X4),
                    lhsT_scale=u_scale_slots[:, t, g, :],
                    rhs=z_tile.bitcast(FP4X4),
                    rhs_scale=z_scale,
                    start=(g == 0),
                    stop=(g == GROUPS - 1),
                )

        def coef_out(c, t):
            nc.scalar.activation(out=coef16[:, t, :], in_=coef_bank[c, t][:], func=COPY, scale=norms32[:, t : t + 1])

        def coef_interleave():
            nc.vector.tensor_copy(
                out=coef_words[:].rearrange("p (n i t) -> p n t i", i=4, t=SLOTS),
                in_=coef16[:].rearrange("p t (n i) -> p n t i", i=4),
            )

        def coef_quantize(c):
            nc.vector.quantize_mx(out=coef_codes[c][:].bitcast(FP8X4), scales=coef_scales[c][:], in_=coef_words[:])


        def ctl_transpose(g):
            pairs = ctl_raw[g][:].bitcast(F32)
            banks = []
            for h in range(2):
                banks.append(bank([P, 2, 2, P]))
                for a in range(2):
                    for u in range(2):
                        nc.tensor.transpose(banks[h][:, a, u, :], pairs[:, 2 * h + a, u : 2 * P : 2], ident[:])
            dst = ctl_words[g % 2][:].bitcast(F32).rearrange("p (h a m u) -> p h a m u", h=2, a=2, u=2)
            for h in range(2):
                nc.scalar.copy(out=dst[:, h], in_=banks[h][:].rearrange("p a u m -> p a m u"))

        def ctl_quantize(g):
            nc.vector.quantize_mx(out=ctl_codes[g][:].bitcast(FP8X4), scales=ctl_scales[g][:], in_=ctl_words[g % 2][:])


        def y_slice(g, c, t, n=1):
            if g in y_rows:
                return y_rows[g][:, t, cols(c, n)]
            return y_chunk[g, c][:, t, :]

        def weighed(g, c, t, n=1):
            return spare.get((g, c, t), y_slice(g, c, t, n))

        def weigh(engine, g, c, t, n=1):
            engine.tensor_scalar(
                out=weighed(g, c, t, n),
                in0=trt[g][:, t, cols(c, n)],
                scalar1=weight32[:, g, t : t + 1],
                scalar2=0.0,
                op0=ALU.mult,
                op1=ALU.add,
            )

        def weigh_on_scalar(g, c, t, n=1):
            nc.scalar.activation(
                out=weighed(g, c, t, n), in_=trt[g][:, t, cols(c, n)], func=COPY, scale=weight32[:, g, t : t + 1]
            )

        def residual(g, c, t):
            fitted = bank([P, CHUNK])
            nc.tensor.matmul_mx(
                out=fitted[:],
                lhsT=ctl_codes[g][:, t * P : (t + 1) * P].bitcast(FP8X4),
                lhsT_scale=ctl_scales[g][:, t * P : (t + 1) * P],
                rhs=coef_codes[c][:].bitcast(FP8X4),
                rhs_scale=coef_scales[c][:],
                start=True,
                stop=True,
            )
            nc.vector.scalar_tensor_tensor(
                out=y_slice(g, c, t),
                in0=fitted[:],
                scalar=minus_weight32[:, g, t : t + 1],
                in1=weighed(g, c, t),
                op0=ALU.mult,
                op1=ALU.add,
            )
            if g in y_rows and c == CHUNKS - 1:
                dst = out_0[rows(g), :].rearrange("(p t) m -> p t m", t=SLOTS)
                nc.sync.dma_start(out=dst[:, t : t + 1, :], in_=y_rows[g][:, t : t + 1, :])

        def stretch(j, first=0, last=STRETCH):
            if first == 0 and j in GPSIMD_WEIGHS:
                spare[GPSIMD_WEIGHS[j][0][:3]] = spare[SLICES[STRETCH * j - 1]]
                for step in GPSIMD_WEIGHS[j]:
                    weigh(nc.gpsimd, *step)
            for n in range(first, last):
                residual(*SLICES[STRETCH * j + n])

        def y_interleave(g, c, first=0, last=CHUNK, copy=nc.scalar.copy):
            whole = y_rows[g][:, :, cols(c)] if g in y_rows else y_chunk[g, c]
            copy(
                out=y_words[g, c][:, first * SLOTS : last * SLOTS].rearrange("p (n i t) -> p n t i", i=2, t=SLOTS),
                in_=whole[:, :, first:last].rearrange("p t (n i) -> p n t i", i=2),
            )

        def y_quantize(g, c):
            nc.vector.quantize_mx(
                out=y_codes[g][:, cols(c)].bitcast(FP8X4),
                scales=y_scales[SCALE_ROWS * g : P, cols(c)],
                in_=y_words[g, c][:],
            )

        def store_y(g, c, src, n=1):
            nc.sync.dma_start(out=out_0[rows(g), cols(c, n)].rearrange("(p t) m -> p t m", t=SLOTS), in_=src)

        def store_codes(g, c, n=1):
            dst = out_1[g].rearrange("p m t -> p (m t)").bitcast(I32)
            nc.sync.dma_start(out=dst[:, cols(c, n)], in_=y_codes[g][:, cols(c, n)].bitcast(I32))

        nc.vector.memset(vectors[:].bitcast(I32), 0)
        nc.vector.memset(z_scale_first[:].bitcast(I32), 0)
        nc.vector.memset(u_scale_raw[:].bitcast(I32), 0)
        nc.vector.memset(z_scale_rest[:].bitcast(I32), 0)
        make_identity(nc, ident[:])

        load_words(u_raw, u_words, 0, N_CTL)
        nc.sync.dma_start(out=vectors[0:GROUPS, :], in_=row_weight.rearrange("(g k) -> g k", g=GROUPS))
        nc.sync.dma_start(out=vectors[GROUPS : GROUPS + 1, :], in_=norms.rearrange("(o k) -> o k", o=1))
        load_scale_rows(u_scale_raw, u_scales, 0, N_CTL)
        load_words(z_first, z_words, 0, CHUNK)
        load_scale_rows(z_scale_first, z_scales, 0, CHUNK)
        load_treatments(0, 0, 2)
        load_controls(0)
        load_treatments(0, 2, 4)
        load_scale_rows(z_scale_rest, z_scales, CHUNK, N_TRT)
        load_words(z_rest, z_words, CHUNK, N_TRT, 0, 2)
        load_words(z_rest, z_words, CHUNK, N_TRT, 2, 4)
        load_controls(1)
        load_treatments(1, 0, 2)
        load_treatments(1, 2, 4)

        vector_bank = bank([P, 2, P])
        for u in range(2):
            nc.tensor.transpose(vector_bank[:, u, :], vectors[:].bitcast(F32)[:, u : 2 * P : 2], ident[:])
        turned = vector_bank[:].bitcast(BF16).rearrange("p u (j e) -> p j u e", e=2)
        nc.scalar.activation(out=norms32[:].rearrange("p (u e) -> p u e", e=2), in_=turned[:, GROUPS], func=COPY)
        nc.scalar.activation(out=weight32[:].rearrange("p g (u e) -> p g u e", e=2), in_=turned[:, :GROUPS], func=COPY)
        nc.scalar.activation(
            out=minus_weight32[:].rearrange("p g (u e) -> p g u e", e=2), in_=turned[:, :GROUPS], func=COPY, scale=-1.0
        )

        for t in range(SLOTS):
            gather_u_slot(t)
        for t in range(SLOTS):
            for c in range(CHUNKS):
                weigh(nc.vector, 0, c, t)
        for t in range(SLOTS):
            coef_passes(0, t)
            coef_out(0, t)
        ctl_transpose(0)
        load_controls(2)
        load_treatments(2)
        coef_interleave()
        ctl_quantize(0)
        coef_quantize(0)

        for t in range(2):
            coef_passes(1, t, 0, 2)
        for t in range(2):
            coef_passes(1, t, 2, 4)
            coef_out(1, t)
        stretch(0)
        ctl_transpose(1)
        weigh(nc.vector, 1, 0, 0)
        weigh(nc.vector, 1, 0, 1)
        ctl_quantize(1)
        weigh(nc.vector, 1, 0, 2)
        weigh(nc.vector, 1, 0, 3)
        weigh(nc.vector, 1, 1, 3)
        for t in range(2):
            weigh_on_scalar(1, 1, t)
            coef_passes(1, 2 + t)
            coef_out(1, 2 + t)
        y_interleave(0, 0)
        stretch(1, 0, 1)
        coef_interleave()
        stretch(1, 1, 2)
        coef_quantize(1)
        stretch(1, 2, 4)

        for t in range(2):
            coef_passes(2, t)
            coef_out(2, t)
        weigh_on_scalar(1, 1, 2)
        load_treatments(3)
        load_controls(3)
        store_y(1, 0, y_chunk[1, 0])
        y_rows[2] = keep.tile([P, SLOTS, N_TRT], F32, name="y_rows2", tag="trt0", align_bytes=64)[:]
        y_interleave(1, 0, 0, HALF)
        stretch(2)
        coef_passes(2, 2)
        coef_passes(2, 3)
        y_quantize(0, 0)
        coef_out(2, 2)
        coef_out(2, 3)
        y_interleave(1, 0, HALF, CHUNK)
        store_y(0, 0, y_pair, 2)
        store_codes(0, 0)
        stretch(3, 0, 3)
        ctl_transpose(2)
        coef_interleave()
        ctl_quantize(2)
        coef_quantize(2)
        stretch(3, 3, 4)
        y_quantize(1, 0)
        store_y(1, 1, y_chunk[1, 1])
        store_codes(1, 0)
        y_interleave(0, 1)
        weigh_on_scalar(1, 2, 2)
        y_interleave(1, 1)

        stretch(4)
        y_quantize(0, 1)
        store_codes(0, 1)
        store_y(0, 2, y_chunk[0, 2])
        weigh_on_scalar(2, 0, 2)
        y_interleave(0, 2)
        stretch(5)
        ctl_transpose(3)
        y_quantize(1, 1)
        store_y(1, 2, y_chunk[1, 2])
        weigh_on_scalar(2, 2, 2)
        y_interleave(1, 2)
        weigh_on_scalar(3, 0, 0, CHUNKS)

        stretch(6)
        y_quantize(0, 2)
        store_codes(0, 2)
        stretch(7)
        ctl_quantize(3)
        stretch(8)
        y_quantize(1, 2)
        store_codes(1, 1, 2)
        for c in range(CHUNKS):
            y_interleave(2, c)

        for c in range(CHUNKS):
            stretch(9 + c)
            y_quantize(2, c)
        store_codes(2, 0, CHUNKS)

        y_interleave(3, 0)
        y_interleave(3, 1, 0, HALF)
        y_interleave(3, 2, 0, CHUNK, nc.vector.tensor_copy)
        y_interleave(3, 1, HALF, CHUNK, nc.vector.tensor_copy)
        y_quantize(3, 0)
        store_codes(3, 0)
        y_quantize(3, 2)
        y_quantize(3, 1)
        store_codes(3, 1, 2)
        for q in range(P // QUADRANT):
            nc.sync.dma_start(
                out=out_2[:, SCALE_ROWS * q : SCALE_ROWS * (q + 1), :].bitcast(I32),
                in_=y_scales[QUADRANT * q : QUADRANT * q + SCALE_ROWS * GROUPS, :].bitcast(I32),
            )
